import numpy as np
import ml_dtypes


def mxq(x, axis, fmt="e4m3"):
    dtype, down = {"e4m3": (ml_dtypes.float8_e4m3fn, 7), "e5m2": (ml_dtypes.float8_e5m2, 14)}[fmt]
    v = np.moveaxis(np.asarray(x, np.float32).astype(ml_dtypes.bfloat16).astype(np.float64), axis, -1)
    blocks = v.reshape(v.shape[:-1] + (-1, 32))
    amax = np.abs(blocks).max(-1, keepdims=True)
    byte = np.maximum(np.where(amax > 0, np.frexp(amax)[1] - 1 + 127, 0) - down, 1)
    scale = np.exp2(byte - 127.0)
    codes = (blocks / scale).astype(np.float32).astype(dtype).astype(np.float64)
    return np.moveaxis((codes * scale).reshape(v.shape), -1, axis)


WIDE = False


def mx_kscale(k):
    if not WIDE:
        return np.ones(k)
    levels = np.array([10, -10, 5, -5, 0])
    if k % 512:
        return np.exp2(np.random.permutation(np.resize(levels, k // 32))).repeat(32)
    a = np.empty((k // 512, 16))
    for p in range(k // 512):
        a[p, :8] = np.random.permutation(np.resize(levels, 8))
        for g in range(8):
            far = levels[np.abs(levels - a[p, g]) >= 10]
            a[p, g + 8] = far[np.random.randint(len(far))]
    return np.exp2(a.ravel()).repeat(32)


def f64(x):
    return np.asarray(x).astype(np.float64)


def striped(idx):
    return np.tile(idx.reshape(-1, 16).T, (8, 1)).astype(np.uint16)


def unstriped(offs):
    return offs[:16].T.reshape(-1).astype(np.int64)


E2M1 = np.array([0.0, 0.5, 1.0, 1.5, 2.0, 3.0, 4.0, 6.0, -0.0, -0.5, -1.0, -1.5, -2.0, -3.0, -4.0, -6.0])


def pack_weight(w, fmt):
    k, n = w.shape
    w = f64(np.asarray(w, np.float32).astype(ml_dtypes.bfloat16)).reshape(k // 32, 32, n)
    amax = np.abs(w).max(1)
    if fmt == "e4m3":
        byte = np.frexp(amax)[1] - 1 + 127 - 7
    else:
        mant, ex = np.frexp(amax / 6.0)
        byte = np.where(mant > 0.5, ex, ex - 1) + 127
    byte = np.clip(np.where(amax > 0, byte, 1), 1, 254)
    scaled = (w * np.exp2(127.0 - byte)[:, None, :]).reshape(k, n).astype(np.float32)
    by_word = np.ascontiguousarray(scaled.reshape(k // 512, 128, 4, n).transpose(0, 1, 3, 2))
    if fmt == "e4m3":
        words = by_word.astype(ml_dtypes.float8_e4m3fn).view(np.uint8)
    else:
        c = by_word.astype(ml_dtypes.float4_e2m1fn).view(np.uint8) & 0xF
        words = (c[..., 0::2] | (c[..., 1::2] << 4)).reshape(k // 512, 128, 2 * n)
    return np.ascontiguousarray(words), np.ascontiguousarray(byte.astype(np.uint8).reshape(k // 512, 16, n))


def unpack_weight(words, scales, fmt):
    g, _, n = scales.shape
    words = np.ascontiguousarray(words).reshape(g, 128, n, -1)
    if fmt == "e4m3":
        vals = words.view(ml_dtypes.float8_e4m3fn).astype(np.float64)
    else:
        nib = np.empty((g, 128, n, 4), np.uint8)
        nib[..., 0::2] = words & 0xF
        nib[..., 1::2] = words >> 4
        vals = E2M1[nib]
    vals = vals * np.repeat(np.exp2(scales.astype(np.float64) - 127.0), 8, axis=1)[..., None]
    return vals.transpose(0, 1, 3, 2).reshape(g * 512, n)


def silu(v):
    return v / (1.0 + np.exp(-np.maximum(v, -700.0)))


def sigmoid(v):
    return 1.0 / (1.0 + np.exp(-np.maximum(v, -700.0)))


K, T, E, C, H, N = 512, 1024, 8, 128, 512, 128


def by_expert(wq, xq):
    return np.concatenate([wq[e].T @ xq[:, e * C:(e + 1) * C] for e in range(E)], axis=1)


def setup_inputs():
    n = np.random.standard_normal
    s = mx_kscale(K)
    u = mx_kscale(H)
    slot_token = np.random.permutation(T)[:E * C]
    x = pack_weight(n((K, T)) * s[:, None], "e4m3")
    wg = pack_weight(n((K, N)) / np.sqrt(K) / s[:, None], "e2m1")
    w1 = [pack_weight(m, "e2m1") for m in n((E, K, H)) / np.sqrt(K) / s[None, :, None] * u]
    w2 = [pack_weight(m, "e2m1") for m in n((E, H, N)) / np.sqrt(H) / u[None, :, None]]
    return {
        "x_words": x[0],
        "x_scales": x[1],
        "wg_words": wg[0],
        "wg_scales": wg[1],
        "w1_words": np.stack([m[0] for m in w1]),
        "w1_scales": np.stack([m[1] for m in w1]),
        "w2_words": np.stack([m[0] for m in w2]),
        "w2_scales": np.stack([m[1] for m in w2]),
        "gate": np.tile(np.random.uniform(0.2, 1.0, E * C), (128, 1)).astype(np.float32),
        "offs": striped(slot_token),
    }


def reference(x_words, x_scales, wg_words, wg_scales, w1_words, w1_scales, w2_words, w2_scales, gate, offs):
    wg = unpack_weight(wg_words, wg_scales, "e2m1")
    w1 = np.stack([unpack_weight(w1_words[e], w1_scales[e], "e2m1") for e in range(E)])
    w2 = np.stack([unpack_weight(w2_words[e], w2_scales[e], "e2m1") for e in range(E)])
    idx = unstriped(offs)
    x = unpack_weight(x_words, x_scales, "e4m3")
    o = sigmoid(wg.T @ x)
    h = silu(by_expert(w1, x[:, idx]))
    y = by_expert(w2, mxq(h, 0, "e4m3"))
    c = np.zeros((N, T))
    c[:, idx] = f64(gate[:1]) * y
    return o * c

@@ -1,0 +1,217 @@
+from contextlib import ExitStack
+
+import concourse.mybir as mybir
+
+K, T, E, C, H, N = 512, 1024, 8, 128, 512, 128
+P = 128
+FLOPS = 2 * K * N * T + 2 * K * H * E * C + 2 * H * N * E * C
+
+F32 = mybir.dt.float32
+BF16 = mybir.dt.bfloat16
+I32 = mybir.dt.int32
+U32 = mybir.dt.uint32
+U16 = mybir.dt.uint16
+U8 = mybir.dt.uint8
+FP8X4 = mybir.dt.float8_e4m3fn_x4
+FP4X4 = mybir.dt.float4_e2m1fn_x4
+ACT = mybir.ActivationFunctionType
+ALU = mybir.AluOpType
+
+W1_GROUPS = (2, 3, 3)
+BYTE_CUTS = (4, 4)
+WORD_CUTS = (1, 1, 2, 2, 2)
+PIECES = (1, 1, 1, 1, 1, 1, 1, 1)
+OUT_CUTS = (256, 256, 256, 256)
+
+
+def runs(sizes):
+    out, at = [], 0
+    for s in sizes:
+        out.append((at, at + s))
+        at = at + s
+    return out
+
+
+def find(cuts, e):
+    for i, (a, b) in enumerate(cuts):
+        if a <= e < b:
+            return i, e - a
+
+
+def tile_moe_ogt_silu_sigmoid_kernel(
+    tc, x_words, x_scales, wg_words, wg_scales, w1_words, w1_scales, w2_words, w2_scales, gate, offs, out
+):
+    nc = tc.nc
+    with ExitStack() as ctx:
+        held = ctx.enter_context(tc.tile_pool(name="held", bufs=1))
+        ring = ctx.enter_context(tc.tile_pool(name="ring", bufs=E))
+        lend = ctx.enter_context(tc.tile_pool(name="lend", bufs=1))
+        psum = ctx.enter_context(tc.psum_pool(name="psum", bufs=1))
+
+        offsets = held.tile([P, T // 16], U16, name="offsets")
+        xw = held.tile([P, T], U32, name="xw", align_bytes=64)
+        xs = held.tile([P, T], U8, name="xs", align_bytes=64)
+        w1s = held.tile([P, E, H], U8, name="w1s", align_bytes=64)
+        w2s = held.tile([P, E, N], U8, name="w2s", align_bytes=64)
+        wgw = held.tile([P, 2 * N], U8, name="wgw", align_bytes=64)
+        wgs = held.tile([P, N], U8, name="wgs", align_bytes=64)
+        ident = held.tile([P, P], F32, name="ident")
+        warm = held.tile([P, 1], F32, name="warm", tag="late", align_bytes=64)
+        warm_out = held.tile([P, 1], F32, name="warm_out")
+        comb = held.tile([P, T], F32, name="comb")
+        groups = runs(W1_GROUPS)
+        zeros = lend.tile([P, E * (2 * H + 2 * N) // 4 + T], F32, name="zeros", align_bytes=64, offset=0)
+
+        nc.gpsimd.memset(xs[:].bitcast(I32), 0)
+        nc.vector.memset(w1s[:].rearrange("p e h -> p (e h)").bitcast(I32), 0)
+        nc.gpsimd.memset(zeros[:, 0:P], 0.0)
+        nc.gpsimd.affine_select(
+            out=ident[:],
+            in_=zeros[:, 0:P],
+            compare_op=ALU.not_equal,
+            fill=1.0,
+            base=0,
+            pattern=[[-1, P]],
+            channel_multiplier=1,
+        )
+        nc.gpsimd.memset(w2s[:].rearrange("p e n -> p (e n)").bitcast(I32), 0)
+        nc.gpsimd.memset(warm[:], 0.0)
+        nc.gpsimd.memset(wgs[:].bitcast(I32), 0)
+        w1w = [
+            lend.tile([P, b - a, 2 * H], U8, name=f"w1w{a}", align_bytes=64, offset=a * 2 * H) for a, b in groups[:-1]
+        ]
+        w2w = lend.tile([P, E, 2 * N], U8, name="w2w", align_bytes=64, offset=E * 2 * H)
+        gate_sb = lend.tile([P, T], F32, name="gate_sb", align_bytes=64, offset=E * (2 * H + 2 * N))
+
+        def rows_2d(queue, plane, src):
+            for r in range(4):
+                queue.dma_start(plane[r:P:32, :].bitcast(I32), src.rearrange("(q r) w -> r q w", r=4)[r].bitcast(I32))
+
+        def rows_3d(queue, plane, src):
+            for r in range(4):
+                queue.dma_start(
+                    plane[r:P:32, :, :].bitcast(I32),
+                    src.rearrange("e s (q r) w -> r q (e s) w", r=4)[r].bitcast(I32),
+                )
+
+        def load_w1(g):
+            a, b = groups[g]
+            nc.sync.dma_start(w1w[g][:].bitcast(I32), w1_words[a:b].rearrange("e s p w -> p (e s) w").bitcast(I32))
+
+        nc.sync.dma_start(offsets[:], offs)
+        nc.sync.dma_start(wgw[:].bitcast(I32), wg_words[0].bitcast(I32))
+        rows_2d(nc.sync, xs, x_scales[0])
+        nc.sync.dma_start(xw[:].bitcast(I32), x_words.rearrange("s p t d -> p (s t d)").bitcast(I32))
+        nc.scalar.activation(warm_out[:], warm[:], ACT.Silu)
+        a, b = groups[-1]
+        w1w.append(held.tile([P, b - a, 2 * H], U8, name="w1w_last", tag="late", align_bytes=64))
+        rows_3d(nc.sync, w1s, w1_scales)
+        load_w1(0)
+        load_w1(1)
+        nc.sync.dma_start(w2w[:].bitcast(I32), w2_words.rearrange("e s p w -> p (e s) w").bitcast(I32))
+        nc.sync.dma_start(gate_sb[:], gate)
+        rows_3d(nc.sync, w2s, w2_scales)
+        load_w1(2)
+        rows_2d(nc.sync, wgs, wg_scales[0])
+
+        byte_cuts, word_cuts = runs(BYTE_CUTS), runs(WORD_CUTS)
+        gs = [held.tile([P, (b - a) * C], U8, name=f"gs{a}", align_bytes=64) for a, b in byte_cuts]
+        gw = [held.tile([P, (b - a) * C], U32, name=f"gw{a}", align_bytes=64) for a, b in word_cuts]
+        per = C // 16
+
+        def gather_for(e):
+            for cuts, dst, src in ((byte_cuts, gs, xs), (word_cuts, gw, xw)):
+                i, j = find(cuts, e)
+                if j == 0:
+                    a, b = cuts[i]
+                    nc.vector.tensor_copy(dst[i][:], src[:].indirect(offsets[:, a * per : b * per]))
+
+        hb = {}
+
+        def first_layer(e):
+            gi, gj = find(groups, e)
+            wi, wj = find(word_cuts, e)
+            bi, bj = find(byte_cuts, e)
+            acc = psum.tile([P, H], F32, name="acc", tag="acc", bufs=4)
+            nc.tensor.matmul_mx(
+                out=acc[:],
+                lhsT=gw[wi][:, wj * C : (wj + 1) * C].bitcast(FP8X4),
+                lhsT_scale=gs[bi][:, bj * C : (bj + 1) * C],
+                rhs=w1w[gi][:, gj, :].bitcast(FP4X4),
+                rhs_scale=w1s[:, e, :],
+                start=True,
+                stop=True,
+            )
+            hb[e] = ring.tile([P, 2, P, 2], BF16, name="hb", tag="hb", align_bytes=64)
+            nc.scalar.activation(hb[e][:], acc[:].rearrange("s (p u d) -> s u p d", u=2, d=2), ACT.Silu)
+
+        codes, planes = {}, {}
+
+        def turn(a, b):
+            n = b - a
+            tr = psum.tile([P, 2, 2, C], F32, name="tr", tag="tr", bufs=2)
+            for e in range(a, b):
+                words = hb[e][:].rearrange("s u p d -> s (u p d)").bitcast(F32)
+                for u in range(2):
+                    nc.tensor.transpose(tr[:, e - a, u, :], words[:, u * P : (u + 1) * P], ident[:])
+            hq = ring.tile([P, n * C * 4], BF16, name="hq", tag="hq", align_bytes=64)
+            nc.scalar.copy(
+                hq[:].bitcast(F32).rearrange("p (j s u) -> p j s u", j=n, u=2),
+                tr[:, 0:n].rearrange("p j u s -> p j s u"),
+            )
+            codes[a] = ring.tile([P, n * C], U32, name="codes", tag="codes", align_bytes=64)
+            planes[a] = ring.tile([P, n * C], U8, name="plane", tag="plane", align_bytes=64)
+            nc.vector.quantize_mx(out=codes[a][:].bitcast(FP8X4), scales=planes[a][:], in_=hq[:])
+
+        def second_layer(a, b):
+            n = b - a
+            y = psum.tile([P, 2 * C], F32, name="y", tag="y", bufs=2)
+            for e in range(a, b):
+                cols = slice((e - a) * C, (e - a + 1) * C)
+                nc.tensor.matmul_mx(
+                    out=y[:, cols],
+                    lhsT=w2w[:, e, :].bitcast(FP4X4),
+                    lhsT_scale=w2s[:, e, :],
+                    rhs=codes[a][:, cols].bitcast(FP8X4),
+                    rhs_scale=planes[a][:, cols],
+                    start=True,
+                    stop=True,
+                )
+            y_sb = ring.tile([P, n * C], F32, name="y_sb", tag="y_sb")
+            nc.scalar.activation(y_sb[:], y[:, 0 : n * C], ACT.Copy, scale=0.5)
+            nc.vector.tensor_tensor(
+                comb[:].indirect(offsets[:, a * per : b * per]), y_sb[:], gate_sb[:, a * C : b * C], ALU.mult
+            )
+
+        pieces = runs(PIECES)
+        for i, (a, b) in enumerate(pieces):
+            for e in range(a, b):
+                gather_for(e)
+                first_layer(e)
+            if i >= 1:
+                turn(*pieces[i - 1])
+            if i >= 2:
+                second_layer(*pieces[i - 2])
+        turn(*pieces[-1])
+        second_layer(*pieces[-2])
+        second_layer(*pieces[-1])
+
+        th = held.tile([P, T], F32, name="th")
+        for h in range(2):
+            cols = slice(h * 512, (h + 1) * 512)
+            og = psum.tile([P, 512], F32, name="og", tag="acc", bufs=4)
+            nc.tensor.matmul_mx(
+                out=og[:],
+                lhsT=wgw[:].bitcast(FP4X4),
+                lhsT_scale=wgs[:],
+                rhs=xw[:, cols].bitcast(FP8X4),
+                rhs_scale=xs[:, cols],
+                start=True,
+                stop=True,
+            )
+            nc.scalar.activation(th[:, cols], og[:], ACT.Tanh, scale=0.5)
+
+        for i, (a, b) in enumerate(runs(OUT_CUTS)):
+            res = held.tile([P, b - a], F32, name=f"res{i}")
+            nc.vector.scalar_tensor_tensor(res[:], th[:, a:b], 1.0, comb[:, a:b], ALU.add, ALU.mult)
+            nc.sync.dma_start(out[:, a:b], res[:])

@@ -1,6 +1,7 @@
 from contextlib import ExitStack
 
 import concourse.mybir as mybir
+from concourse.masks import make_identity
 
 K, T, E, C, H, N = 512, 1024, 8, 128, 512, 128
 P = 128
@@ -17,10 +18,11 @@ FP4X4 = mybir.dt.float4_e2m1fn_x4
 ACT = mybir.ActivationFunctionType
 ALU = mybir.AluOpType
 
-W1_GROUPS = (2, 3, 3)
-BYTE_CUTS = (4, 4)
+W1_GROUPS = (3, 2, 3)
+BYTE_CUTS = (5, 3)
 WORD_CUTS = (1, 1, 2, 2, 2)
 PIECES = (1, 1, 1, 1, 1, 1, 1, 1)
+GATE_CUTS = (2, 6)
 OUT_CUTS = (256, 256, 256, 256)
 
 
@@ -52,43 +54,47 @@ def tile_moe_ogt_silu_sigmoid_kernel(
         xw = held.tile([P, T], U32, name="xw", align_bytes=64)
         xs = held.tile([P, T], U8, name="xs", align_bytes=64)
         w1s = held.tile([P, E, H], U8, name="w1s", align_bytes=64)
-        w2s = held.tile([P, E, N], U8, name="w2s", align_bytes=64)
-        wgw = held.tile([P, 2 * N], U8, name="wgw", align_bytes=64)
-        wgs = held.tile([P, N], U8, name="wgs", align_bytes=64)
         ident = held.tile([P, P], F32, name="ident")
-        warm = held.tile([P, 1], F32, name="warm", tag="late", align_bytes=64)
-        warm_out = held.tile([P, 1], F32, name="warm_out")
         comb = held.tile([P, T], F32, name="comb")
         groups = runs(W1_GROUPS)
-        zeros = lend.tile([P, E * (2 * H + 2 * N) // 4 + T], F32, name="zeros", align_bytes=64, offset=0)
+        w2s = held.tile([P, E, N], U8, name="w2s", align_bytes=64)
+        warm_out = held.tile([P, 1], F32, name="warm_out")
+        late_bytes = (E - W1_GROUPS[0]) * 2 * H + E * 2 * N + 4 * T + 2 * N + N
+        warm = lend.tile([P, late_bytes // 4], F32, name="warm", align_bytes=64, offset=0)
 
         nc.gpsimd.memset(xs[:].bitcast(I32), 0)
         nc.vector.memset(w1s[:].rearrange("p e h -> p (e h)").bitcast(I32), 0)
-        nc.gpsimd.memset(zeros[:, 0:P], 0.0)
-        nc.gpsimd.affine_select(
-            out=ident[:],
-            in_=zeros[:, 0:P],
-            compare_op=ALU.not_equal,
-            fill=1.0,
-            base=0,
-            pattern=[[-1, P]],
-            channel_multiplier=1,
-        )
-        nc.gpsimd.memset(w2s[:].rearrange("p e n -> p (e n)").bitcast(I32), 0)
-        nc.gpsimd.memset(warm[:], 0.0)
-        nc.gpsimd.memset(wgs[:].bitcast(I32), 0)
-        w1w = [
-            lend.tile([P, b - a, 2 * H], U8, name=f"w1w{a}", align_bytes=64, offset=a * 2 * H) for a, b in groups[:-1]
+        nc.vector.memset(w2s[:].rearrange("p e n -> p (e n)").bitcast(I32), 0)
+        nc.vector.memset(warm[:, 0:1], 0.0)
+        make_identity(nc, ident[:])
+        nc.scalar.activation(warm_out[:], warm[:, 0:1], ACT.Silu)
+
+        w1w = [held.tile([P, W1_GROUPS[0], 2 * H], U8, name="w1w0", align_bytes=64)]
+        for a, b in groups[1:]:
+            at = (a - W1_GROUPS[0]) * 2 * H
+            w1w.append(lend.tile([P, b - a, 2 * H], U8, name=f"w1w{a}", align_bytes=64, offset=at))
+        at = (E - W1_GROUPS[0]) * 2 * H
+        w2w = lend.tile([P, E, 2 * N], U8, name="w2w", align_bytes=64, offset=at)
+        at = at + E * 2 * N
+        gate_cuts = runs(GATE_CUTS)
+        gate_sb = [
+            lend.tile([P, (b - a) * C], F32, name=f"gate{a}", align_bytes=64, offset=at + a * C * 4) for a, b in gate_cuts
         ]
-        w2w = lend.tile([P, E, 2 * N], U8, name="w2w", align_bytes=64, offset=E * 2 * H)
-        gate_sb = lend.tile([P, T], F32, name="gate_sb", align_bytes=64, offset=E * (2 * H + 2 * N))
+        at = at + 4 * T
+        wgw = lend.tile([P, 2 * N], U8, name="wgw", align_bytes=64, offset=at)
+        wgs = lend.tile([P, N], U8, name="wgs", align_bytes=64, offset=at + 2 * N)
+        nc.gpsimd.memset(wgs[:].bitcast(I32), 0)
+
+        def load_gate(g):
+            a, b = gate_cuts[g]
+            nc.sync.dma_start(gate_sb[g][:], gate[:, a * C : b * C])
 
         def rows_2d(queue, plane, src):
             for r in range(4):
                 queue.dma_start(plane[r:P:32, :].bitcast(I32), src.rearrange("(q r) w -> r q w", r=4)[r].bitcast(I32))
 
-        def rows_3d(queue, plane, src):
-            for r in range(4):
+        def rows_3d(queue, plane, src, rows=range(4)):
+            for r in rows:
                 queue.dma_start(
                     plane[r:P:32, :, :].bitcast(I32),
                     src.rearrange("e s (q r) w -> r q (e s) w", r=4)[r].bitcast(I32),
@@ -96,35 +102,37 @@ def tile_moe_ogt_silu_sigmoid_kernel(
 
         def load_w1(g):
             a, b = groups[g]
-            nc.sync.dma_start(w1w[g][:].bitcast(I32), w1_words[a:b].rearrange("e s p w -> p (e s) w").bitcast(I32))
+            nc.sync.dma_start(w1w[g][:].bitcast(I32), w1_words.bitcast(I32)[a:b, 0].rearrange("e p w -> p e w"))
 
         nc.sync.dma_start(offsets[:], offs)
-        nc.sync.dma_start(wgw[:].bitcast(I32), wg_words[0].bitcast(I32))
+        load_w1(0)
         rows_2d(nc.sync, xs, x_scales[0])
         nc.sync.dma_start(xw[:].bitcast(I32), x_words.rearrange("s p t d -> p (s t d)").bitcast(I32))
-        nc.scalar.activation(warm_out[:], warm[:], ACT.Silu)
-        a, b = groups[-1]
-        w1w.append(held.tile([P, b - a, 2 * H], U8, name="w1w_last", tag="late", align_bytes=64))
         rows_3d(nc.sync, w1s, w1_scales)
-        load_w1(0)
-        load_w1(1)
-        nc.sync.dma_start(w2w[:].bitcast(I32), w2_words.rearrange("e s p w -> p (e s) w").bitcast(I32))
-        nc.sync.dma_start(gate_sb[:], gate)
         rows_3d(nc.sync, w2s, w2_scales)
+        nc.sync.dma_start(w2w[:].bitcast(I32), w2_words.rearrange("e s p w -> p (e s) w").bitcast(I32))
+        load_gate(0)
+        load_w1(1)
         load_w1(2)
+        load_gate(1)
+        nc.sync.dma_start(wgw[:].bitcast(I32), wg_words[0].bitcast(I32))
         rows_2d(nc.sync, wgs, wg_scales[0])
 
         byte_cuts, word_cuts = runs(BYTE_CUTS), runs(WORD_CUTS)
-        gs = [held.tile([P, (b - a) * C], U8, name=f"gs{a}", align_bytes=64) for a, b in byte_cuts]
-        gw = [held.tile([P, (b - a) * C], U32, name=f"gw{a}", align_bytes=64) for a, b in word_cuts]
+        gs, gw = {}, {}
         per = C // 16
 
         def gather_for(e):
-            for cuts, dst, src in ((byte_cuts, gs, xs), (word_cuts, gw, xw)):
-                i, j = find(cuts, e)
-                if j == 0:
-                    a, b = cuts[i]
-                    nc.vector.tensor_copy(dst[i][:], src[:].indirect(offsets[:, a * per : b * per]))
+            i, j = find(byte_cuts, e)
+            if j == 0:
+                a, b = byte_cuts[i]
+                gs[i] = held.tile([P, (b - a) * C], U8, name="gs", tag="reused" if i == 1 else "gs", align_bytes=64)
+                nc.vector.tensor_copy(gs[i][:], xs[:].indirect(offsets[:, a * per : b * per]))
+            i, j = find(word_cuts, e)
+            if j == 0:
+                a, b = word_cuts[i]
+                gw[i] = held.tile([P, (b - a) * C], U32, name="gw", tag=f"gw{i}", align_bytes=64)
+                nc.vector.tensor_copy(gw[i][:], xw[:].indirect(offsets[:, a * per : b * per]))
 
         hb = {}
 
@@ -132,7 +140,7 @@ def tile_moe_ogt_silu_sigmoid_kernel(
             gi, gj = find(groups, e)
             wi, wj = find(word_cuts, e)
             bi, bj = find(byte_cuts, e)
-            acc = psum.tile([P, H], F32, name="acc", tag="acc", bufs=4)
+            acc = psum.tile([P, H], F32, name="acc", tag=f"bank{e % 2 if e < 4 else (e + 2) % 4}")
             nc.tensor.matmul_mx(
                 out=acc[:],
                 lhsT=gw[wi][:, wj * C : (wj + 1) * C].bitcast(FP8X4),
@@ -149,23 +157,23 @@ def tile_moe_ogt_silu_sigmoid_kernel(
 
         def turn(a, b):
             n = b - a
-            tr = psum.tile([P, 2, 2, C], F32, name="tr", tag="tr", bufs=2)
+            tr = psum.tile([P, 2, 2, C], F32, name="tr", tag="tr", bufs=3)
             for e in range(a, b):
                 words = hb[e][:].rearrange("s u p d -> s (u p d)").bitcast(F32)
                 for u in range(2):
                     nc.tensor.transpose(tr[:, e - a, u, :], words[:, u * P : (u + 1) * P], ident[:])
-            hq = ring.tile([P, n * C * 4], BF16, name="hq", tag="hq", align_bytes=64)
+            hq = held.tile([P, n * C * 4], BF16, name="hq", tag="reused" if a == 0 else f"hq{a}", align_bytes=64)
             nc.scalar.copy(
                 hq[:].bitcast(F32).rearrange("p (j s u) -> p j s u", j=n, u=2),
                 tr[:, 0:n].rearrange("p j u s -> p j s u"),
             )
-            codes[a] = ring.tile([P, n * C], U32, name="codes", tag="codes", align_bytes=64)
+            codes[a] = held.tile([P, n * C], U32, name="codes", tag=f"slot{a}", align_bytes=64)
             planes[a] = ring.tile([P, n * C], U8, name="plane", tag="plane", align_bytes=64)
             nc.vector.quantize_mx(out=codes[a][:].bitcast(FP8X4), scales=planes[a][:], in_=hq[:])
 
         def second_layer(a, b):
             n = b - a
-            y = psum.tile([P, 2 * C], F32, name="y", tag="y", bufs=2)
+            y = psum.tile([P, H], F32, name="y", tag=f"bank{(a + 2) % 4}")
             for e in range(a, b):
                 cols = slice((e - a) * C, (e - a + 1) * C)
                 nc.tensor.matmul_mx(
@@ -177,10 +185,14 @@ def tile_moe_ogt_silu_sigmoid_kernel(
                     start=True,
                     stop=True,
                 )
-            y_sb = ring.tile([P, n * C], F32, name="y_sb", tag="y_sb")
-            nc.scalar.activation(y_sb[:], y[:, 0 : n * C], ACT.Copy, scale=0.5)
+            y_sb = held.tile([P, n * C], F32, name="y_sb", tag=f"slot{a + 3}", align_bytes=64)
+            if a < 4:
+                nc.vector.tensor_scalar_mul(y_sb[:], y[:, 0 : n * C], 0.5)
+            else:
+                nc.scalar.activation(y_sb[:], y[:, 0 : n * C], ACT.Copy, scale=0.5)
+            gi, gj = find(gate_cuts, a)
             nc.vector.tensor_tensor(
-                comb[:].indirect(offsets[:, a * per : b * per]), y_sb[:], gate_sb[:, a * C : b * C], ALU.mult
+                comb[:].indirect(offsets[:, a * per : b * per]), y_sb[:], gate_sb[gi][:, gj * C : (gj + n) * C], ALU.mult
             )
 
         pieces = runs(PIECES)
@@ -199,7 +211,7 @@ def tile_moe_ogt_silu_sigmoid_kernel(
         th = held.tile([P, T], F32, name="th")
         for h in range(2):
             cols = slice(h * 512, (h + 1) * 512)
-            og = psum.tile([P, 512], F32, name="og", tag="acc", bufs=4)
+            og = psum.tile([P, 512], F32, name="og", tag=f"bank{h + 2}")
             nc.tensor.matmul_mx(
                 out=og[:],
                 lhsT=wgw[:].bitcast(FP4X4),

@@ -18,212 +18,216 @@ FP4X4 = mybir.dt.float4_e2m1fn_x4
 ACT = mybir.ActivationFunctionType
 ALU = mybir.AluOpType
 
-W1_GROUPS = (3, 2, 3)
-BYTE_CUTS = (5, 3)
-WORD_CUTS = (1, 1, 2, 2, 2)
-PIECES = (1, 1, 1, 1, 1, 1, 1, 1)
-GATE_CUTS = (2, 6)
-OUT_CUTS = (256, 256, 256, 256)
+BANK = 512
+ALIGN = 64
+LIST_COLS = C // 16
+
+W1_LOADS = (3, 2, 3)
+GATE_LOADS = (2, 6)
+BYTE_GATHERS = (5, 3)
+WORD_GATHERS = (1, 1, 2, 2, 2)
+TURNS_ON_VECTOR = 1
+RESULTS_ON_VECTOR = 4
+FIRST_BANKS = 4
+RUN_AHEAD = 3
+OUT_COLS = 256
 
 
-def runs(sizes):
-    out, at = [], 0
-    for s in sizes:
-        out.append((at, at + s))
-        at = at + s
-    return out
+def ranges(sizes):
+    ends = [sum(sizes[: i + 1]) for i in range(len(sizes))]
+    return [(end - size, end) for size, end in zip(sizes, ends)]
 
 
-def find(cuts, e):
-    for i, (a, b) in enumerate(cuts):
-        if a <= e < b:
-            return i, e - a
+def locate(cuts, e):
+    piece = [first <= e < end for first, end in cuts].index(True)
+    return piece, e - cuts[piece][0]
 
 
 def tile_moe_ogt_silu_sigmoid_kernel(
     tc, x_words, x_scales, wg_words, wg_scales, w1_words, w1_scales, w2_words, w2_scales, gate, offs, out
 ):
     nc = tc.nc
+    w1_cuts, gate_cuts = ranges(W1_LOADS), ranges(GATE_LOADS)
+    byte_cuts, word_cuts = ranges(BYTE_GATHERS), ranges(WORD_GATHERS)
+
     with ExitStack() as ctx:
         held = ctx.enter_context(tc.tile_pool(name="held", bufs=1))
-        ring = ctx.enter_context(tc.tile_pool(name="ring", bufs=E))
-        lend = ctx.enter_context(tc.tile_pool(name="lend", bufs=1))
+        late = ctx.enter_context(tc.tile_pool(name="late", bufs=1))
         psum = ctx.enter_context(tc.psum_pool(name="psum", bufs=1))
 
         offsets = held.tile([P, T // 16], U16, name="offsets")
-        xw = held.tile([P, T], U32, name="xw", align_bytes=64)
-        xs = held.tile([P, T], U8, name="xs", align_bytes=64)
-        w1s = held.tile([P, E, H], U8, name="w1s", align_bytes=64)
+        x_w = held.tile([P, T], U32, name="x_w", align_bytes=ALIGN)
+        x_plane = held.tile([P, T], U8, name="x_plane", align_bytes=ALIGN)
+        w1_plane = held.tile([P, E, H], U8, name="w1_plane", align_bytes=ALIGN)
+        w2_plane = held.tile([P, E, N], U8, name="w2_plane", align_bytes=ALIGN)
         ident = held.tile([P, P], F32, name="ident")
-        comb = held.tile([P, T], F32, name="comb")
-        groups = runs(W1_GROUPS)
-        w2s = held.tile([P, E, N], U8, name="w2s", align_bytes=64)
-        warm_out = held.tile([P, 1], F32, name="warm_out")
-        late_bytes = (E - W1_GROUPS[0]) * 2 * H + E * 2 * N + 4 * T + 2 * N + N
-        warm = lend.tile([P, late_bytes // 4], F32, name="warm", align_bytes=64, offset=0)
+        combined = held.tile([P, T], F32, name="combined")
+        zero_bias = held.tile([P, 1], F32, name="zero_bias")
 
-        nc.gpsimd.memset(xs[:].bitcast(I32), 0)
-        nc.vector.memset(w1s[:].rearrange("p e h -> p (e h)").bitcast(I32), 0)
-        nc.vector.memset(w2s[:].rearrange("p e n -> p (e n)").bitcast(I32), 0)
-        nc.vector.memset(warm[:, 0:1], 0.0)
+        nc.gpsimd.memset(x_plane[:].bitcast(I32), 0)
+        nc.vector.memset(w1_plane[:].rearrange("p e h -> p (e h)").bitcast(I32), 0)
+        nc.vector.memset(w2_plane[:].rearrange("p e n -> p (e n)").bitcast(I32), 0)
+
+        late_bytes = (E - W1_LOADS[0]) * 2 * H + E * 2 * N + 4 * T + 2 * N + N
+        zero_src = late.tile([P, late_bytes // 4], F32, name="zero_src", align_bytes=ALIGN, offset=0)
+        nc.vector.memset(zero_src[:, 0:1], 0.0)
         make_identity(nc, ident[:])
-        nc.scalar.activation(warm_out[:], warm[:, 0:1], ACT.Silu)
+        nc.scalar.activation(zero_bias[:], zero_src[:, 0:1], ACT.Silu)
 
-        w1w = [held.tile([P, W1_GROUPS[0], 2 * H], U8, name="w1w0", align_bytes=64)]
-        for a, b in groups[1:]:
-            at = (a - W1_GROUPS[0]) * 2 * H
-            w1w.append(lend.tile([P, b - a, 2 * H], U8, name=f"w1w{a}", align_bytes=64, offset=at))
-        at = (E - W1_GROUPS[0]) * 2 * H
-        w2w = lend.tile([P, E, 2 * N], U8, name="w2w", align_bytes=64, offset=at)
+        w1_w = [held.tile([P, W1_LOADS[0], 2 * H], U8, name="w1_w0", align_bytes=ALIGN)]
+        at = 0
+        for first, end in w1_cuts[1:]:
+            w1_w.append(late.tile([P, end - first, 2 * H], U8, name=f"w1_w{first}", align_bytes=ALIGN, offset=at))
+            at = at + (end - first) * 2 * H
+        w2_w = late.tile([P, E, 2 * N], U8, name="w2_w", align_bytes=ALIGN, offset=at)
         at = at + E * 2 * N
-        gate_cuts = runs(GATE_CUTS)
-        gate_sb = [
-            lend.tile([P, (b - a) * C], F32, name=f"gate{a}", align_bytes=64, offset=at + a * C * 4) for a, b in gate_cuts
-        ]
-        at = at + 4 * T
-        wgw = lend.tile([P, 2 * N], U8, name="wgw", align_bytes=64, offset=at)
-        wgs = lend.tile([P, N], U8, name="wgs", align_bytes=64, offset=at + 2 * N)
-        nc.gpsimd.memset(wgs[:].bitcast(I32), 0)
+        gate_sb = []
+        for first, end in gate_cuts:
+            gate_sb.append(late.tile([P, (end - first) * C], F32, name=f"gate{first}", align_bytes=ALIGN, offset=at))
+            at = at + (end - first) * C * 4
+        wg_w = late.tile([P, 2 * N], U8, name="wg_w", align_bytes=ALIGN, offset=at)
+        wg_plane = late.tile([P, N], U8, name="wg_plane", align_bytes=ALIGN, offset=at + 2 * N)
+        nc.gpsimd.memset(wg_plane[:].bitcast(I32), 0)
 
-        def load_gate(g):
-            a, b = gate_cuts[g]
-            nc.sync.dma_start(gate_sb[g][:], gate[:, a * C : b * C])
-
-        def rows_2d(queue, plane, src):
+        def load_plane(plane, rows):
             for r in range(4):
-                queue.dma_start(plane[r:P:32, :].bitcast(I32), src.rearrange("(q r) w -> r q w", r=4)[r].bitcast(I32))
+                nc.sync.dma_start(plane[r:P:32, :].bitcast(I32), rows.rearrange("(q r) w -> r q w", r=4)[r].bitcast(I32))
 
-        def rows_3d(queue, plane, src, rows=range(4)):
-            for r in rows:
-                queue.dma_start(
+        def load_expert_planes(plane, rows):
+            for r in range(4):
+                nc.sync.dma_start(
                     plane[r:P:32, :, :].bitcast(I32),
-                    src.rearrange("e s (q r) w -> r q (e s) w", r=4)[r].bitcast(I32),
+                    rows.rearrange("e s (q r) w -> r q (e s) w", r=4)[r].bitcast(I32),
                 )
 
-        def load_w1(g):
-            a, b = groups[g]
-            nc.sync.dma_start(w1w[g][:].bitcast(I32), w1_words.bitcast(I32)[a:b, 0].rearrange("e p w -> p e w"))
+        def load_w1(piece):
+            first, end = w1_cuts[piece]
+            nc.sync.dma_start(
+                w1_w[piece][:].bitcast(I32), w1_words.bitcast(I32)[first:end, 0].rearrange("e p w -> p e w")
+            )
+
+        def load_gate(piece):
+            first, end = gate_cuts[piece]
+            nc.sync.dma_start(gate_sb[piece][:], gate[:, first * C : end * C])
 
         nc.sync.dma_start(offsets[:], offs)
         load_w1(0)
-        rows_2d(nc.sync, xs, x_scales[0])
-        nc.sync.dma_start(xw[:].bitcast(I32), x_words.rearrange("s p t d -> p (s t d)").bitcast(I32))
-        rows_3d(nc.sync, w1s, w1_scales)
-        rows_3d(nc.sync, w2s, w2_scales)
-        nc.sync.dma_start(w2w[:].bitcast(I32), w2_words.rearrange("e s p w -> p (e s) w").bitcast(I32))
+        load_plane(x_plane, x_scales[0])
+        nc.sync.dma_start(x_w[:].bitcast(I32), x_words.rearrange("s p t d -> p (s t d)").bitcast(I32))
+        load_expert_planes(w1_plane, w1_scales)
+        load_expert_planes(w2_plane, w2_scales)
+        nc.sync.dma_start(w2_w[:].bitcast(I32), w2_words.rearrange("e s p w -> p (e s) w").bitcast(I32))
         load_gate(0)
         load_w1(1)
         load_w1(2)
         load_gate(1)
-        nc.sync.dma_start(wgw[:].bitcast(I32), wg_words[0].bitcast(I32))
-        rows_2d(nc.sync, wgs, wg_scales[0])
+        nc.sync.dma_start(wg_w[:].bitcast(I32), wg_words[0].bitcast(I32))
+        load_plane(wg_plane, wg_scales[0])
 
-        byte_cuts, word_cuts = runs(BYTE_CUTS), runs(WORD_CUTS)
-        gs, gw = {}, {}
-        per = C // 16
+        slot_planes, slot_words, h_pairs, h_codes, h_planes = {}, {}, {}, {}, {}
 
-        def gather_for(e):
-            i, j = find(byte_cuts, e)
-            if j == 0:
-                a, b = byte_cuts[i]
-                gs[i] = held.tile([P, (b - a) * C], U8, name="gs", tag="reused" if i == 1 else "gs", align_bytes=64)
-                nc.vector.tensor_copy(gs[i][:], xs[:].indirect(offsets[:, a * per : b * per]))
-            i, j = find(word_cuts, e)
-            if j == 0:
-                a, b = word_cuts[i]
-                gw[i] = held.tile([P, (b - a) * C], U32, name="gw", tag=f"gw{i}", align_bytes=64)
-                nc.vector.tensor_copy(gw[i][:], xw[:].indirect(offsets[:, a * per : b * per]))
-
-        hb = {}
+        def gather(e):
+            piece, place = locate(byte_cuts, e)
+            if place == 0:
+                first, end = byte_cuts[piece]
+                slot_planes[piece] = held.tile(
+                    [P, (end - first) * C], U8, name="slot_plane", tag="h_turned0" if piece else "slot_plane", align_bytes=ALIGN
+                )
+                nc.vector.tensor_copy(
+                    slot_planes[piece][:], x_plane[:].indirect(offsets[:, first * LIST_COLS : end * LIST_COLS])
+                )
+            piece, place = locate(word_cuts, e)
+            if place == 0:
+                first, end = word_cuts[piece]
+                slot_words[piece] = held.tile([P, (end - first) * C], U32, name=f"slot_words{piece}", align_bytes=ALIGN)
+                nc.vector.tensor_copy(
+                    slot_words[piece][:], x_w[:].indirect(offsets[:, first * LIST_COLS : end * LIST_COLS])
+                )
 
         def first_layer(e):
-            gi, gj = find(groups, e)
-            wi, wj = find(word_cuts, e)
-            bi, bj = find(byte_cuts, e)
-            acc = psum.tile([P, H], F32, name="acc", tag=f"bank{e % 2 if e < 4 else (e + 2) % 4}")
+            w1_piece, w1_place = locate(w1_cuts, e)
+            word_piece, word_place = locate(word_cuts, e)
+            byte_piece, byte_place = locate(byte_cuts, e)
+            pre = psum.tile([P, H], F32, name="pre", tag=f"first{e % FIRST_BANKS}")
             nc.tensor.matmul_mx(
-                out=acc[:],
-                lhsT=gw[wi][:, wj * C : (wj + 1) * C].bitcast(FP8X4),
-                lhsT_scale=gs[bi][:, bj * C : (bj + 1) * C],
-                rhs=w1w[gi][:, gj, :].bitcast(FP4X4),
-                rhs_scale=w1s[:, e, :],
+                out=pre[:],
+                lhsT=slot_words[word_piece][:, word_place * C : (word_place + 1) * C].bitcast(FP8X4),
+                lhsT_scale=slot_planes[byte_piece][:, byte_place * C : (byte_place + 1) * C],
+                rhs=w1_w[w1_piece][:, w1_place, :].bitcast(FP4X4),
+                rhs_scale=w1_plane[:, e, :],
                 start=True,
                 stop=True,
             )
-            hb[e] = ring.tile([P, 2, P, 2], BF16, name="hb", tag="hb", align_bytes=64)
-            nc.scalar.activation(hb[e][:], acc[:].rearrange("s (p u d) -> s u p d", u=2, d=2), ACT.Silu)
-
-        codes, planes = {}, {}
-
-        def turn(a, b):
-            n = b - a
-            tr = psum.tile([P, 2, 2, C], F32, name="tr", tag="tr", bufs=3)
-            for e in range(a, b):
-                words = hb[e][:].rearrange("s u p d -> s (u p d)").bitcast(F32)
-                for u in range(2):
-                    nc.tensor.transpose(tr[:, e - a, u, :], words[:, u * P : (u + 1) * P], ident[:])
-            hq = held.tile([P, n * C * 4], BF16, name="hq", tag="reused" if a == 0 else f"hq{a}", align_bytes=64)
-            nc.scalar.copy(
-                hq[:].bitcast(F32).rearrange("p (j s u) -> p j s u", j=n, u=2),
-                tr[:, 0:n].rearrange("p j u s -> p j s u"),
+            h_pairs[e] = held.tile([P, 2, P, 2], BF16, name=f"h_pairs{e}", align_bytes=ALIGN)
+            nc.scalar.activation(
+                h_pairs[e][:], pre[:].rearrange("s (p u d) -> s u p d", u=2, d=2), ACT.Silu, bias=zero_bias[:]
             )
-            codes[a] = held.tile([P, n * C], U32, name="codes", tag=f"slot{a}", align_bytes=64)
-            planes[a] = ring.tile([P, n * C], U8, name="plane", tag="plane", align_bytes=64)
-            nc.vector.quantize_mx(out=codes[a][:].bitcast(FP8X4), scales=planes[a][:], in_=hq[:])
 
-        def second_layer(a, b):
-            n = b - a
-            y = psum.tile([P, H], F32, name="y", tag=f"bank{(a + 2) % 4}")
-            for e in range(a, b):
-                cols = slice((e - a) * C, (e - a + 1) * C)
-                nc.tensor.matmul_mx(
-                    out=y[:, cols],
-                    lhsT=w2w[:, e, :].bitcast(FP4X4),
-                    lhsT_scale=w2s[:, e, :],
-                    rhs=codes[a][:, cols].bitcast(FP8X4),
-                    rhs_scale=planes[a][:, cols],
-                    start=True,
-                    stop=True,
-                )
-            y_sb = held.tile([P, n * C], F32, name="y_sb", tag=f"slot{a + 3}", align_bytes=64)
-            if a < 4:
-                nc.vector.tensor_scalar_mul(y_sb[:], y[:, 0 : n * C], 0.5)
+        def turn_and_quantise(e):
+            turned = psum.tile([P, 2, C], F32, name="turned", tag="turned", bufs=2)
+            pairs = h_pairs[e][:].rearrange("s u p d -> s (u p d)").bitcast(F32)
+            for u in range(2):
+                nc.tensor.transpose(turned[:, u, :], pairs[:, u * P : (u + 1) * P], ident[:])
+            h_turned = held.tile([P, C * 4], BF16, name="h_turned", tag=f"h_turned{e}", align_bytes=ALIGN)
+            move = nc.vector.tensor_copy if e < TURNS_ON_VECTOR else nc.scalar.copy
+            move(h_turned[:].bitcast(F32).rearrange("p (s u) -> p s u", u=2), turned[:].rearrange("p u s -> p s u"))
+            h_codes[e] = held.tile([P, C], U32, name="h_codes", tag=f"shared{e}", align_bytes=ALIGN)
+            h_planes[e] = held.tile([P, C], U8, name=f"h_plane{e}", align_bytes=ALIGN)
+            nc.vector.quantize_mx(out=h_codes[e][:].bitcast(FP8X4), scales=h_planes[e][:], in_=h_turned[:])
+
+        def second_layer(e):
+            y = psum.tile([P, C], F32, name="y", tag="y", bufs=2)
+            nc.tensor.matmul_mx(
+                out=y[:],
+                lhsT=w2_w[:, e, :].bitcast(FP4X4),
+                lhsT_scale=w2_plane[:, e, :],
+                rhs=h_codes[e][:].bitcast(FP8X4),
+                rhs_scale=h_planes[e][:],
+                start=True,
+                stop=True,
+            )
+            y_half = held.tile([P, C], F32, name="y_half", tag=f"shared{e + RUN_AHEAD}", align_bytes=ALIGN)
+            if e < RESULTS_ON_VECTOR:
+                nc.vector.tensor_scalar_mul(y_half[:], y[:], 0.5)
             else:
-                nc.scalar.activation(y_sb[:], y[:, 0 : n * C], ACT.Copy, scale=0.5)
-            gi, gj = find(gate_cuts, a)
+                nc.scalar.activation(y_half[:], y[:], ACT.Copy, scale=0.5)
+            piece, place = locate(gate_cuts, e)
             nc.vector.tensor_tensor(
-                comb[:].indirect(offsets[:, a * per : b * per]), y_sb[:], gate_sb[gi][:, gj * C : (gj + n) * C], ALU.mult
+                combined[:].indirect(offsets[:, e * LIST_COLS : (e + 1) * LIST_COLS]),
+                y_half[:],
+                gate_sb[piece][:, place * C : (place + 1) * C],
+                ALU.mult,
             )
 
-        pieces = runs(PIECES)
-        for i, (a, b) in enumerate(pieces):
-            for e in range(a, b):
-                gather_for(e)
-                first_layer(e)
-            if i >= 1:
-                turn(*pieces[i - 1])
-            if i >= 2:
-                second_layer(*pieces[i - 2])
-        turn(*pieces[-1])
-        second_layer(*pieces[-2])
-        second_layer(*pieces[-1])
+        for step in range(E + 2):
+            if step < E:
+                gather(step)
+                first_layer(step)
+            if 1 <= step <= E:
+                turn_and_quantise(step - 1)
+            if step >= 2:
+                second_layer(step - 2)
 
-        th = held.tile([P, T], F32, name="th")
-        for h in range(2):
-            cols = slice(h * 512, (h + 1) * 512)
-            og = psum.tile([P, 512], F32, name="og", tag=f"bank{h + 2}")
+        gate_tanh = held.tile([P, T], F32, name="gate_tanh")
+        gate_banks = (
+            psum.tile([P, BANK], F32, name="gate_pre0", tag=f"first{(E - 1) % FIRST_BANKS}"),
+            psum.tile([P, BANK], F32, name="gate_pre1", tag="turned", bufs=2),
+        )
+        for half, gate_pre in enumerate(gate_banks):
+            cols = slice(half * BANK, (half + 1) * BANK)
             nc.tensor.matmul_mx(
-                out=og[:],
-                lhsT=wgw[:].bitcast(FP4X4),
-                lhsT_scale=wgs[:],
-                rhs=xw[:, cols].bitcast(FP8X4),
-                rhs_scale=xs[:, cols],
+                out=gate_pre[:],
+                lhsT=wg_w[:].bitcast(FP4X4),
+                lhsT_scale=wg_plane[:],
+                rhs=x_w[:, cols].bitcast(FP8X4),
+                rhs_scale=x_plane[:, cols],
                 start=True,
                 stop=True,
             )
-            nc.scalar.activation(th[:, cols], og[:], ACT.Tanh, scale=0.5)
+            nc.scalar.activation(gate_tanh[:, cols], gate_pre[:], ACT.Tanh, bias=zero_bias[:], scale=0.5)
 
-        for i, (a, b) in enumerate(runs(OUT_CUTS)):
-            res = held.tile([P, b - a], F32, name=f"res{i}")
-            nc.vector.scalar_tensor_tensor(res[:], th[:, a:b], 1.0, comb[:, a:b], ALU.add, ALU.mult)
-            nc.sync.dma_start(out[:, a:b], res[:])
+        for first in range(0, T, OUT_COLS):
+            cols = slice(first, first + OUT_COLS)
+            result = held.tile([P, OUT_COLS], F32, name=f"result{first}")
+            nc.vector.scalar_tensor_tensor(result[:], gate_tanh[:, cols], 1.0, combined[:, cols], ALU.add, ALU.mult)
+            nc.sync.dma_start(out[:, cols], result[:])

@@ -21,15 +21,20 @@ ALU = mybir.AluOpType
 BANK = 512
 ALIGN = 64
 LIST_COLS = C // 16
+PAIR = 2
+PAIRS = E // PAIR
 
-W1_LOADS = (3, 2, 3)
+W1_LOADS = (2, 3, 3)
 GATE_LOADS = (2, 6)
 BYTE_GATHERS = (5, 3)
 WORD_GATHERS = (1, 1, 2, 2, 2)
-TURNS_ON_VECTOR = 1
-RESULTS_ON_VECTOR = 4
 FIRST_BANKS = 4
-RUN_AHEAD = 3
+FIRST_AHEAD = 2
+TURNS_ON_VECTOR = 2
+RESULTS_ON_VECTOR = 1
+TURN_BANK = ("a", "b", "c", "a")
+RESULT_BANK = ("c", "b", "c", "a")
+WARM_PASSES = 2
 OUT_COLS = 256
 
 
@@ -52,7 +57,6 @@ def tile_moe_ogt_silu_sigmoid_kernel(
 
     with ExitStack() as ctx:
         held = ctx.enter_context(tc.tile_pool(name="held", bufs=1))
-        late = ctx.enter_context(tc.tile_pool(name="late", bufs=1))
         psum = ctx.enter_context(tc.psum_pool(name="psum", bufs=1))
 
         offsets = held.tile([P, T // 16], U16, name="offsets")
@@ -60,45 +64,38 @@ def tile_moe_ogt_silu_sigmoid_kernel(
         x_plane = held.tile([P, T], U8, name="x_plane", align_bytes=ALIGN)
         w1_plane = held.tile([P, E, H], U8, name="w1_plane", align_bytes=ALIGN)
         w2_plane = held.tile([P, E, N], U8, name="w2_plane", align_bytes=ALIGN)
+        wg_plane = held.tile([P, N], U8, name="wg_plane", align_bytes=ALIGN)
         ident = held.tile([P, P], F32, name="ident")
         combined = held.tile([P, T], F32, name="combined")
+        zero_src = held.tile([P, 1], F32, name="zero_src")
         zero_bias = held.tile([P, 1], F32, name="zero_bias")
+        w1_w = [
+            held.tile([P, end - first, 2 * H], U8, name=f"w1_w{first}", align_bytes=ALIGN) for first, end in w1_cuts
+        ]
+        w2_w = held.tile([P, E, 2 * N], U8, name="w2_w", align_bytes=ALIGN)
+        gate_sb = [held.tile([P, (end - first) * C], F32, name=f"gate{first}") for first, end in gate_cuts]
+        wg_w = held.tile([P, 2 * N], U8, name="wg_w", align_bytes=ALIGN)
 
-        nc.gpsimd.memset(x_plane[:].bitcast(I32), 0)
-        nc.vector.memset(w1_plane[:].rearrange("p e h -> p (e h)").bitcast(I32), 0)
-        nc.vector.memset(w2_plane[:].rearrange("p e n -> p (e n)").bitcast(I32), 0)
-
-        late_bytes = (E - W1_LOADS[0]) * 2 * H + E * 2 * N + 4 * T + 2 * N + N
-        zero_src = late.tile([P, late_bytes // 4], F32, name="zero_src", align_bytes=ALIGN, offset=0)
-        nc.vector.memset(zero_src[:, 0:1], 0.0)
+        nc.gpsimd.memset(zero_src[:], 0.0)
+        nc.scalar.activation(zero_bias[:], zero_src[:], ACT.Silu)
         make_identity(nc, ident[:])
-        nc.scalar.activation(zero_bias[:], zero_src[:, 0:1], ACT.Silu)
 
-        w1_w = [held.tile([P, W1_LOADS[0], 2 * H], U8, name="w1_w0", align_bytes=ALIGN)]
-        at = 0
-        for first, end in w1_cuts[1:]:
-            w1_w.append(late.tile([P, end - first, 2 * H], U8, name=f"w1_w{first}", align_bytes=ALIGN, offset=at))
-            at = at + (end - first) * 2 * H
-        w2_w = late.tile([P, E, 2 * N], U8, name="w2_w", align_bytes=ALIGN, offset=at)
-        at = at + E * 2 * N
-        gate_sb = []
-        for first, end in gate_cuts:
-            gate_sb.append(late.tile([P, (end - first) * C], F32, name=f"gate{first}", align_bytes=ALIGN, offset=at))
-            at = at + (end - first) * C * 4
-        wg_w = late.tile([P, 2 * N], U8, name="wg_w", align_bytes=ALIGN, offset=at)
-        wg_plane = late.tile([P, N], U8, name="wg_plane", align_bytes=ALIGN, offset=at + 2 * N)
-        nc.gpsimd.memset(wg_plane[:].bitcast(I32), 0)
-
-        def load_plane(plane, rows):
-            for r in range(4):
-                nc.sync.dma_start(plane[r:P:32, :].bitcast(I32), rows.rearrange("(q r) w -> r q w", r=4)[r].bitcast(I32))
-
-        def load_expert_planes(plane, rows):
-            for r in range(4):
+        def load_token_plane():
+            rows = x_scales[0].bitcast(I32)
+            for q in range(4):
                 nc.sync.dma_start(
-                    plane[r:P:32, :, :].bitcast(I32),
-                    rows.rearrange("e s (q r) w -> r q (e s) w", r=4)[r].bitcast(I32),
+                    x_plane[32 * q : 32 * (q + 1), :].bitcast(I32), rows[4 * q : 4 * (q + 1), :].partition_broadcast(8)
                 )
+
+        def load_gate_plane():
+            rows = wg_scales[0].rearrange("(q r) w -> r q w", r=4)
+            for r in range(4):
+                nc.sync.dma_start(wg_plane[r:P:32, :].bitcast(I32), rows[r].bitcast(I32))
+
+        def load_expert_planes(plane, scales):
+            rows = scales.rearrange("e s (q r) w -> r q (e s) w", r=4)
+            for r in range(4):
+                nc.sync.dma_start(plane[r:P:32, :, :].bitcast(I32), rows[r].bitcast(I32))
 
         def load_w1(piece):
             first, end = w1_cuts[piece]
@@ -111,44 +108,47 @@ def tile_moe_ogt_silu_sigmoid_kernel(
             nc.sync.dma_start(gate_sb[piece][:], gate[:, first * C : end * C])
 
         nc.sync.dma_start(offsets[:], offs)
-        load_w1(0)
-        load_plane(x_plane, x_scales[0])
+        load_token_plane()
         nc.sync.dma_start(x_w[:].bitcast(I32), x_words.rearrange("s p t d -> p (s t d)").bitcast(I32))
-        load_expert_planes(w1_plane, w1_scales)
-        load_expert_planes(w2_plane, w2_scales)
-        nc.sync.dma_start(w2_w[:].bitcast(I32), w2_words.rearrange("e s p w -> p (e s) w").bitcast(I32))
-        load_gate(0)
-        load_w1(1)
-        load_w1(2)
-        load_gate(1)
         nc.sync.dma_start(wg_w[:].bitcast(I32), wg_words[0].bitcast(I32))
-        load_plane(wg_plane, wg_scales[0])
+        load_expert_planes(w1_plane, w1_scales)
+        for piece in range(len(W1_LOADS)):
+            load_w1(piece)
+        load_expert_planes(w2_plane, w2_scales)
+        load_gate(0)
+        nc.sync.dma_start(w2_w[:].bitcast(I32), w2_words.rearrange("e s p w -> p (e s) w").bitcast(I32))
+        load_gate(1)
+        load_gate_plane()
 
-        slot_planes, slot_words, h_pairs, h_codes, h_planes = {}, {}, {}, {}, {}
+        slot_planes, slot_words, h_couples, turned, h_turned, h_codes, h_planes, y, y_half, gate_tanh = [
+            {} for i in range(10)
+        ]
 
         def gather(e):
             piece, place = locate(byte_cuts, e)
             if place == 0:
                 first, end = byte_cuts[piece]
-                slot_planes[piece] = held.tile(
-                    [P, (end - first) * C], U8, name="slot_plane", tag="h_turned0" if piece else "slot_plane", align_bytes=ALIGN
-                )
+                tag = "slot_words0" if piece else "slot_plane"
+                slot_planes[piece] = held.tile([P, (end - first) * C], U8, name="slot_plane", tag=tag, align_bytes=ALIGN)
                 nc.vector.tensor_copy(
                     slot_planes[piece][:], x_plane[:].indirect(offsets[:, first * LIST_COLS : end * LIST_COLS])
                 )
             piece, place = locate(word_cuts, e)
             if place == 0:
                 first, end = word_cuts[piece]
-                slot_words[piece] = held.tile([P, (end - first) * C], U32, name=f"slot_words{piece}", align_bytes=ALIGN)
+                slot_words[piece] = held.tile(
+                    [P, (end - first) * C], U32, name="slot_words", tag=f"slot_words{piece}", align_bytes=ALIGN
+                )
                 nc.vector.tensor_copy(
                     slot_words[piece][:], x_w[:].indirect(offsets[:, first * LIST_COLS : end * LIST_COLS])
                 )
 
         def first_layer(e):
+            gather(e)
             w1_piece, w1_place = locate(w1_cuts, e)
             word_piece, word_place = locate(word_cuts, e)
             byte_piece, byte_place = locate(byte_cuts, e)
-            pre = psum.tile([P, H], F32, name="pre", tag=f"first{e % FIRST_BANKS}")
+            pre = psum.tile([P, H], F32, name="pre", tag="pre", bufs=FIRST_BANKS)
             nc.tensor.matmul_mx(
                 out=pre[:],
                 lhsT=slot_words[word_piece][:, word_place * C : (word_place + 1) * C].bitcast(FP8X4),
@@ -158,63 +158,68 @@ def tile_moe_ogt_silu_sigmoid_kernel(
                 start=True,
                 stop=True,
             )
-            h_pairs[e] = held.tile([P, 2, P, 2], BF16, name=f"h_pairs{e}", align_bytes=ALIGN)
+            tag = "h_plane0" if e == E - PAIR else f"h_couples{e}"
+            h_couples[e] = held.tile([P, 2, P, 2], BF16, name="h_couples", tag=tag, align_bytes=ALIGN)
             nc.scalar.activation(
-                h_pairs[e][:], pre[:].rearrange("s (p u d) -> s u p d", u=2, d=2), ACT.Silu, bias=zero_bias[:]
+                h_couples[e][:], pre[:].rearrange("s (p u d) -> s u p d", u=2, d=2), ACT.Silu, bias=zero_bias[:]
             )
 
-        def turn_and_quantise(e):
-            turned = psum.tile([P, 2, C], F32, name="turned", tag="turned", bufs=2)
-            pairs = h_pairs[e][:].rearrange("s u p d -> s (u p d)").bitcast(F32)
+        def turn(e):
+            g, place = divmod(e, PAIR)
+            if place == 0:
+                turned[g] = psum.tile([P, PAIR, 2, C], F32, name="turned", tag=TURN_BANK[g])
+            words = h_couples[e][:].rearrange("s u p d -> s (u p d)").bitcast(F32)
             for u in range(2):
-                nc.tensor.transpose(turned[:, u, :], pairs[:, u * P : (u + 1) * P], ident[:])
-            h_turned = held.tile([P, C * 4], BF16, name="h_turned", tag=f"h_turned{e}", align_bytes=ALIGN)
-            move = nc.vector.tensor_copy if e < TURNS_ON_VECTOR else nc.scalar.copy
-            move(h_turned[:].bitcast(F32).rearrange("p (s u) -> p s u", u=2), turned[:].rearrange("p u s -> p s u"))
-            h_codes[e] = held.tile([P, C], U32, name="h_codes", tag=f"shared{e}", align_bytes=ALIGN)
-            h_planes[e] = held.tile([P, C], U8, name=f"h_plane{e}", align_bytes=ALIGN)
-            nc.vector.quantize_mx(out=h_codes[e][:].bitcast(FP8X4), scales=h_planes[e][:], in_=h_turned[:])
+                nc.tensor.transpose(turned[g][:, place, u, :], words[:, u * P : (u + 1) * P], ident[:])
 
-        def second_layer(e):
-            y = psum.tile([P, C], F32, name="y", tag="y", bufs=2)
-            nc.tensor.matmul_mx(
-                out=y[:],
-                lhsT=w2_w[:, e, :].bitcast(FP4X4),
-                lhsT_scale=w2_plane[:, e, :],
-                rhs=h_codes[e][:].bitcast(FP8X4),
-                rhs_scale=h_planes[e][:],
-                start=True,
-                stop=True,
+        def lay_out(g):
+            tag = "h_codes0" if g == PAIRS - 1 else f"h_turned{g}"
+            h_turned[g] = held.tile([P, PAIR * C * 4], BF16, name="h_turned", tag=tag, align_bytes=ALIGN)
+            move = nc.vector.tensor_copy if g < TURNS_ON_VECTOR else nc.scalar.copy
+            move(
+                h_turned[g][:].bitcast(F32).rearrange("p (e s u) -> p e s u", s=C, u=2),
+                turned[g][:].rearrange("p e u s -> p e s u"),
             )
-            y_half = held.tile([P, C], F32, name="y_half", tag=f"shared{e + RUN_AHEAD}", align_bytes=ALIGN)
-            if e < RESULTS_ON_VECTOR:
-                nc.vector.tensor_scalar_mul(y_half[:], y[:], 0.5)
+
+        def quantise(g):
+            tag = "h_codes0" if g == 1 else f"h_codes{g}"
+            h_codes[g] = held.tile([P, PAIR * C], U32, name="h_codes", tag=tag, align_bytes=ALIGN)
+            h_planes[g] = held.tile([P, PAIR * C], U8, name="h_plane", tag=f"h_plane{g}", align_bytes=ALIGN)
+            nc.vector.quantize_mx(out=h_codes[g][:].bitcast(FP8X4), scales=h_planes[g][:], in_=h_turned[g][:])
+
+        def second_layer(g):
+            y[g] = psum.tile([P, PAIR * C], F32, name="y", tag=RESULT_BANK[g])
+            for place in range(PAIR):
+                e, cols = PAIR * g + place, slice(place * C, (place + 1) * C)
+                nc.tensor.matmul_mx(
+                    out=y[g][:, cols],
+                    lhsT=w2_w[:, e, :].bitcast(FP4X4),
+                    lhsT_scale=w2_plane[:, e, :],
+                    rhs=h_codes[g][:, cols].bitcast(FP8X4),
+                    rhs_scale=h_planes[g][:, cols],
+                    start=True,
+                    stop=True,
+                )
+            tag = f"h_couples{PAIR * (g + 2) - 1}"
+            y_half[g] = held.tile([P, PAIR * C], F32, name="y_half", tag=tag, align_bytes=ALIGN)
+            if g < RESULTS_ON_VECTOR:
+                nc.vector.tensor_scalar_mul(y_half[g][:], y[g][:], 0.5)
             else:
-                nc.scalar.activation(y_half[:], y[:], ACT.Copy, scale=0.5)
-            piece, place = locate(gate_cuts, e)
+                nc.scalar.activation(y_half[g][:], y[g][:], ACT.Copy, scale=0.5)
+
+        def scatter(g):
+            first, end = PAIR * g, PAIR * (g + 1)
+            piece, place = locate(gate_cuts, first)
             nc.vector.tensor_tensor(
-                combined[:].indirect(offsets[:, e * LIST_COLS : (e + 1) * LIST_COLS]),
-                y_half[:],
-                gate_sb[piece][:, place * C : (place + 1) * C],
+                combined[:].indirect(offsets[:, first * LIST_COLS : end * LIST_COLS]),
+                y_half[g][:],
+                gate_sb[piece][:, place * C : (place + PAIR) * C],
                 ALU.mult,
             )
 
-        for step in range(E + 2):
-            if step < E:
-                gather(step)
-                first_layer(step)
-            if 1 <= step <= E:
-                turn_and_quantise(step - 1)
-            if step >= 2:
-                second_layer(step - 2)
-
-        gate_tanh = held.tile([P, T], F32, name="gate_tanh")
-        gate_banks = (
-            psum.tile([P, BANK], F32, name="gate_pre0", tag=f"first{(E - 1) % FIRST_BANKS}"),
-            psum.tile([P, BANK], F32, name="gate_pre1", tag="turned", bufs=2),
-        )
-        for half, gate_pre in enumerate(gate_banks):
+        def output_gate(half, tag):
             cols = slice(half * BANK, (half + 1) * BANK)
+            gate_pre = psum.tile([P, BANK], F32, name="gate_pre", tag="pre", bufs=FIRST_BANKS)
             nc.tensor.matmul_mx(
                 out=gate_pre[:],
                 lhsT=wg_w[:].bitcast(FP4X4),
@@ -224,10 +229,45 @@ def tile_moe_ogt_silu_sigmoid_kernel(
                 start=True,
                 stop=True,
             )
-            nc.scalar.activation(gate_tanh[:, cols], gate_pre[:], ACT.Tanh, bias=zero_bias[:], scale=0.5)
+            gate_tanh[half] = held.tile([P, BANK], F32, name="gate_tanh", tag=tag, align_bytes=ALIGN)
+            nc.scalar.activation(gate_tanh[half][:], gate_pre[:], ACT.Tanh, bias=zero_bias[:], scale=0.5)
+
+        warm = psum.tile([P, BANK], F32, name="warm", tag=RESULT_BANK[0])
+        for i in range(WARM_PASSES):
+            nc.tensor.matmul_mx(
+                out=warm[:],
+                lhsT=wg_w[:].bitcast(FP4X4),
+                lhsT_scale=x_plane[:, 0:N],
+                rhs=x_w[:, 0:BANK].bitcast(FP8X4),
+                rhs_scale=x_plane[:, 0:BANK],
+                start=True,
+                stop=True,
+            )
+
+        for e in range(FIRST_AHEAD):
+            first_layer(e)
+        for g in range(PAIRS):
+            for e in range(PAIR * g, PAIR * (g + 1)):
+                if e + FIRST_AHEAD < E:
+                    first_layer(e + FIRST_AHEAD)
+                turn(e)
+            lay_out(g)
+            if g > 0:
+                second_layer(g - 1)
+            quantise(g)
+            if g > 0:
+                scatter(g - 1)
+        second_layer(PAIRS - 1)
+        scatter(PAIRS - 1)
+
+        output_gate(0, f"h_codes{PAIRS - 1}")
+        output_gate(1, f"h_plane{PAIRS - 1}")
 
         for first in range(0, T, OUT_COLS):
+            half, at = divmod(first, BANK)
             cols = slice(first, first + OUT_COLS)
             result = held.tile([P, OUT_COLS], F32, name=f"result{first}")
-            nc.vector.scalar_tensor_tensor(result[:], gate_tanh[:, cols], 1.0, combined[:, cols], ALU.add, ALU.mult)
+            nc.vector.scalar_tensor_tensor(
+                result[:], gate_tanh[half][:, at : at + OUT_COLS], 1.0, combined[:, cols], ALU.add, ALU.mult
+            )
             nc.sync.dma_start(out[:, cols], result[:])

@@ -34,7 +34,6 @@ TURNS_ON_VECTOR = 2
 RESULTS_ON_VECTOR = 1
 TURN_BANK = ("a", "b", "c", "a")
 RESULT_BANK = ("c", "b", "c", "a")
-WARM_PASSES = 2
 OUT_COLS = 256
 
 
@@ -110,7 +109,6 @@ def tile_moe_ogt_silu_sigmoid_kernel(
         nc.sync.dma_start(offsets[:], offs)
         load_token_plane()
         nc.sync.dma_start(x_w[:].bitcast(I32), x_words.rearrange("s p t d -> p (s t d)").bitcast(I32))
-        nc.sync.dma_start(wg_w[:].bitcast(I32), wg_words[0].bitcast(I32))
         load_expert_planes(w1_plane, w1_scales)
         for piece in range(len(W1_LOADS)):
             load_w1(piece)
@@ -118,6 +116,7 @@ def tile_moe_ogt_silu_sigmoid_kernel(
         load_gate(0)
         nc.sync.dma_start(w2_w[:].bitcast(I32), w2_words.rearrange("e s p w -> p (e s) w").bitcast(I32))
         load_gate(1)
+        nc.sync.dma_start(wg_w[:].bitcast(I32), wg_words[0].bitcast(I32))
         load_gate_plane()
 
         slot_planes, slot_words, h_couples, turned, h_turned, h_codes, h_planes, y, y_half, gate_tanh = [
@@ -231,18 +230,6 @@ def tile_moe_ogt_silu_sigmoid_kernel(
             )
             gate_tanh[half] = held.tile([P, BANK], F32, name="gate_tanh", tag=tag, align_bytes=ALIGN)
             nc.scalar.activation(gate_tanh[half][:], gate_pre[:], ACT.Tanh, bias=zero_bias[:], scale=0.5)
-
-        warm = psum.tile([P, BANK], F32, name="warm", tag=RESULT_BANK[0])
-        for i in range(WARM_PASSES):
-            nc.tensor.matmul_mx(
-                out=warm[:],
-                lhsT=wg_w[:].bitcast(FP4X4),
-                lhsT_scale=x_plane[:, 0:N],
-                rhs=x_w[:, 0:BANK].bitcast(FP8X4),
-                rhs_scale=x_plane[:, 0:BANK],
-                start=True,
-                stop=True,
-            )
 
         for e in range(FIRST_AHEAD):
             first_layer(e)

@@ -24,7 +24,7 @@ LIST_COLS = C // 16
 PAIR = 2
 PAIRS = E // PAIR
 
-W1_LOADS = (2, 3, 3)
+W1_LOADS = (1, 2, 2, 3)
 GATE_LOADS = (2, 6)
 BYTE_GATHERS = (5, 3)
 WORD_GATHERS = (1, 1, 2, 2, 2)
@@ -147,7 +147,8 @@ def tile_moe_ogt_silu_sigmoid_kernel(
             w1_piece, w1_place = locate(w1_cuts, e)
             word_piece, word_place = locate(word_cuts, e)
             byte_piece, byte_place = locate(byte_cuts, e)
-            pre = psum.tile([P, H], F32, name="pre", tag="pre", bufs=FIRST_BANKS)
+            bank = e if e < FIRST_BANKS else 1 + (e - 1) % (FIRST_BANKS - 1)
+            pre = psum.tile([P, H], F32, name="pre", tag=f"first{bank}")
             nc.tensor.matmul_mx(
                 out=pre[:],
                 lhsT=slot_words[word_piece][:, word_place * C : (word_place + 1) * C].bitcast(FP8X4),
@@ -218,7 +219,7 @@ def tile_moe_ogt_silu_sigmoid_kernel(
 
         def output_gate(half, tag):
             cols = slice(half * BANK, (half + 1) * BANK)
-            gate_pre = psum.tile([P, BANK], F32, name="gate_pre", tag="pre", bufs=FIRST_BANKS)
+            gate_pre = psum.tile([P, BANK], F32, name="gate_pre", tag=f"first{2 * half}")
             nc.tensor.matmul_mx(
                 out=gate_pre[:],
                 lhsT=wg_w[:].bitcast(FP4X4),

@@ -34,6 +34,7 @@ TURNS_ON_VECTOR = 2
 RESULTS_ON_VECTOR = 1
 TURN_BANK = ("a", "b", "c", "a")
 RESULT_BANK = ("c", "b", "c", "a")
+WARM_PASSES = 2
 OUT_COLS = 256
 
 
@@ -109,6 +110,7 @@ def tile_moe_ogt_silu_sigmoid_kernel(
         nc.sync.dma_start(offsets[:], offs)
         load_token_plane()
         nc.sync.dma_start(x_w[:].bitcast(I32), x_words.rearrange("s p t d -> p (s t d)").bitcast(I32))
+        nc.sync.dma_start(wg_w[:].bitcast(I32), wg_words[0].bitcast(I32))
         load_expert_planes(w1_plane, w1_scales)
         for piece in range(len(W1_LOADS)):
             load_w1(piece)
@@ -116,7 +118,6 @@ def tile_moe_ogt_silu_sigmoid_kernel(
         load_gate(0)
         nc.sync.dma_start(w2_w[:].bitcast(I32), w2_words.rearrange("e s p w -> p (e s) w").bitcast(I32))
         load_gate(1)
-        nc.sync.dma_start(wg_w[:].bitcast(I32), wg_words[0].bitcast(I32))
         load_gate_plane()
 
         slot_planes, slot_words, h_couples, turned, h_turned, h_codes, h_planes, y, y_half, gate_tanh = [
@@ -231,6 +232,18 @@ def tile_moe_ogt_silu_sigmoid_kernel(
             )
             gate_tanh[half] = held.tile([P, BANK], F32, name="gate_tanh", tag=tag, align_bytes=ALIGN)
             nc.scalar.activation(gate_tanh[half][:], gate_pre[:], ACT.Tanh, bias=zero_bias[:], scale=0.5)
+
+        warm = psum.tile([P, BANK], F32, name="warm", tag=RESULT_BANK[0])
+        for i in range(WARM_PASSES):
+            nc.tensor.matmul_mx(
+                out=warm[:],
+                lhsT=wg_w[:].bitcast(FP4X4),
+                lhsT_scale=x_plane[:, 0:N],
+                rhs=x_w[:, 0:BANK].bitcast(FP8X4),
+                rhs_scale=x_plane[:, 0:BANK],
+                start=True,
+                stop=True,
+            )
 
         for e in range(FIRST_AHEAD):
             first_layer(e)

@@ -21,20 +21,19 @@ ALU = mybir.AluOpType
 BANK = 512
 ALIGN = 64
 LIST_COLS = C // 16
-PAIR = 2
-PAIRS = E // PAIR
 
-W1_LOADS = (1, 2, 2, 3)
+W1_LOADS = (1, 2, 3, 2)
 GATE_LOADS = (2, 6)
-BYTE_GATHERS = (5, 3)
+BYTE_GATHERS = (4, 4)
 WORD_GATHERS = (1, 1, 2, 2, 2)
+GROUPS = (2, 2, 2, 2)
+TURNS = (1, 1, 1, 1, 2, 2)
 FIRST_BANKS = 4
-FIRST_AHEAD = 2
-TURNS_ON_VECTOR = 2
+TURNS_ON_VECTOR = 4
 RESULTS_ON_VECTOR = 1
-TURN_BANK = ("a", "b", "c", "a")
-RESULT_BANK = ("c", "b", "c", "a")
-WARM_PASSES = 2
+TURN_BANK = ("a", "d", "b", "a", "c", "a")
+RESULT_BANK = ("c", "d", "b", "c")
+GATE_BANK = ("first0", "first2")
 OUT_COLS = 256
 
 
@@ -53,6 +52,7 @@ def tile_moe_ogt_silu_sigmoid_kernel(
 ):
     nc = tc.nc
     w1_cuts, gate_cuts = ranges(W1_LOADS), ranges(GATE_LOADS)
+    groups, turns = ranges(GROUPS), ranges(TURNS)
     byte_cuts, word_cuts = ranges(BYTE_GATHERS), ranges(WORD_GATHERS)
 
     with ExitStack() as ctx:
@@ -78,6 +78,7 @@ def tile_moe_ogt_silu_sigmoid_kernel(
 
         nc.gpsimd.memset(zero_src[:], 0.0)
         nc.scalar.activation(zero_bias[:], zero_src[:], ACT.Silu)
+        nc.gpsimd.dma_start(wg_w[:].bitcast(I32), wg_words[0].bitcast(I32))
         make_identity(nc, ident[:])
 
         def load_token_plane():
@@ -110,13 +111,14 @@ def tile_moe_ogt_silu_sigmoid_kernel(
         nc.sync.dma_start(offsets[:], offs)
         load_token_plane()
         nc.sync.dma_start(x_w[:].bitcast(I32), x_words.rearrange("s p t d -> p (s t d)").bitcast(I32))
-        nc.sync.dma_start(wg_w[:].bitcast(I32), wg_words[0].bitcast(I32))
+        load_w1(0)
         load_expert_planes(w1_plane, w1_scales)
-        for piece in range(len(W1_LOADS)):
+        for piece in range(1, len(W1_LOADS) - 1):
             load_w1(piece)
         load_expert_planes(w2_plane, w2_scales)
-        load_gate(0)
         nc.sync.dma_start(w2_w[:].bitcast(I32), w2_words.rearrange("e s p w -> p (e s) w").bitcast(I32))
+        load_w1(len(W1_LOADS) - 1)
+        load_gate(0)
         load_gate(1)
         load_gate_plane()
 
@@ -124,27 +126,20 @@ def tile_moe_ogt_silu_sigmoid_kernel(
             {} for i in range(10)
         ]
 
-        def gather(e):
-            piece, place = locate(byte_cuts, e)
-            if place == 0:
-                first, end = byte_cuts[piece]
-                tag = "slot_words0" if piece else "slot_plane"
-                slot_planes[piece] = held.tile([P, (end - first) * C], U8, name="slot_plane", tag=tag, align_bytes=ALIGN)
-                nc.vector.tensor_copy(
-                    slot_planes[piece][:], x_plane[:].indirect(offsets[:, first * LIST_COLS : end * LIST_COLS])
-                )
-            piece, place = locate(word_cuts, e)
-            if place == 0:
-                first, end = word_cuts[piece]
-                slot_words[piece] = held.tile(
-                    [P, (end - first) * C], U32, name="slot_words", tag=f"slot_words{piece}", align_bytes=ALIGN
-                )
-                nc.vector.tensor_copy(
-                    slot_words[piece][:], x_w[:].indirect(offsets[:, first * LIST_COLS : end * LIST_COLS])
-                )
+        def list_slice(first, end):
+            return offsets[:, first * LIST_COLS : end * LIST_COLS]
+
+        def gather_bytes(piece, tag):
+            first, end = byte_cuts[piece]
+            slot_planes[piece] = held.tile([P, (end - first) * C], U8, name="slot_plane", tag=tag, align_bytes=ALIGN)
+            nc.vector.tensor_copy(slot_planes[piece][:], x_plane[:].indirect(list_slice(first, end)))
+
+        def gather_words(piece, tag):
+            first, end = word_cuts[piece]
+            slot_words[piece] = held.tile([P, (end - first) * C], U32, name="slot_words", tag=tag, align_bytes=ALIGN)
+            nc.vector.tensor_copy(slot_words[piece][:], x_w[:].indirect(list_slice(first, end)))
 
         def first_layer(e):
-            gather(e)
             w1_piece, w1_place = locate(w1_cuts, e)
             word_piece, word_place = locate(word_cuts, e)
             byte_piece, byte_place = locate(byte_cuts, e)
@@ -159,41 +154,47 @@ def tile_moe_ogt_silu_sigmoid_kernel(
                 start=True,
                 stop=True,
             )
-            tag = "h_plane0" if e == E - PAIR else f"h_couples{e}"
-            h_couples[e] = held.tile([P, 2, P, 2], BF16, name="h_couples", tag=tag, align_bytes=ALIGN)
+            h_couples[e] = held.tile([P, 2, P, 2], BF16, name="h_couples", tag=f"h_couples{e}", align_bytes=ALIGN)
             nc.scalar.activation(
                 h_couples[e][:], pre[:].rearrange("s (p u d) -> s u p d", u=2, d=2), ACT.Silu, bias=zero_bias[:]
             )
 
-        def turn(e):
-            g, place = divmod(e, PAIR)
-            if place == 0:
-                turned[g] = psum.tile([P, PAIR, 2, C], F32, name="turned", tag=TURN_BANK[g])
-            words = h_couples[e][:].rearrange("s u p d -> s (u p d)").bitcast(F32)
-            for u in range(2):
-                nc.tensor.transpose(turned[g][:, place, u, :], words[:, u * P : (u + 1) * P], ident[:])
+        def turn(g):
+            first, end = turns[g]
+            size = end - first
+            turned[g] = psum.tile([P, size, 2, C], F32, name="turned", tag=TURN_BANK[g])
+            for e in range(first, end):
+                words = h_couples[e][:].rearrange("s u p d -> s (u p d)").bitcast(F32)
+                for u in range(2):
+                    nc.tensor.transpose(turned[g][:, e - first, u, :], words[:, u * P : (u + 1) * P], ident[:])
 
         def lay_out(g):
-            tag = "h_codes0" if g == PAIRS - 1 else f"h_turned{g}"
-            h_turned[g] = held.tile([P, PAIR * C * 4], BF16, name="h_turned", tag=tag, align_bytes=ALIGN)
+            first, end = turns[g]
+            group, place = locate(groups, first)
+            if place == 0:
+                h_turned[group] = held.tile(
+                    [P, GROUPS[group] * H], BF16, name="h_turned", tag=f"h_turned{group}", align_bytes=ALIGN
+                )
+            laid = h_turned[group][:, place * H : (place + end - first) * H]
             move = nc.vector.tensor_copy if g < TURNS_ON_VECTOR else nc.scalar.copy
             move(
-                h_turned[g][:].bitcast(F32).rearrange("p (e s u) -> p e s u", s=C, u=2),
+                laid.bitcast(F32).rearrange("p (e s u) -> p e s u", s=C, u=2),
                 turned[g][:].rearrange("p e u s -> p e s u"),
             )
 
-        def quantise(g):
-            tag = "h_codes0" if g == 1 else f"h_codes{g}"
-            h_codes[g] = held.tile([P, PAIR * C], U32, name="h_codes", tag=tag, align_bytes=ALIGN)
-            h_planes[g] = held.tile([P, PAIR * C], U8, name="h_plane", tag=f"h_plane{g}", align_bytes=ALIGN)
+        def quantise(g, tag):
+            first, end = groups[g]
+            h_codes[g] = held.tile([P, (end - first) * C], U32, name="h_codes", tag=tag, align_bytes=ALIGN)
+            h_planes[g] = held.tile([P, (end - first) * C], U8, name="h_plane", tag=f"h_plane{g}", align_bytes=ALIGN)
             nc.vector.quantize_mx(out=h_codes[g][:].bitcast(FP8X4), scales=h_planes[g][:], in_=h_turned[g][:])
 
-        def second_layer(g):
-            y[g] = psum.tile([P, PAIR * C], F32, name="y", tag=RESULT_BANK[g])
-            for place in range(PAIR):
-                e, cols = PAIR * g + place, slice(place * C, (place + 1) * C)
+        def second_layer(g, tag):
+            first, end = groups[g]
+            y = psum.tile([P, (end - first) * C], F32, name="y", tag=RESULT_BANK[g])
+            for e in range(first, end):
+                cols = slice((e - first) * C, (e - first + 1) * C)
                 nc.tensor.matmul_mx(
-                    out=y[g][:, cols],
+                    out=y[:, cols],
                     lhsT=w2_w[:, e, :].bitcast(FP4X4),
                     lhsT_scale=w2_plane[:, e, :],
                     rhs=h_codes[g][:, cols].bitcast(FP8X4),
@@ -201,26 +202,25 @@ def tile_moe_ogt_silu_sigmoid_kernel(
                     start=True,
                     stop=True,
                 )
-            tag = f"h_couples{PAIR * (g + 2) - 1}"
-            y_half[g] = held.tile([P, PAIR * C], F32, name="y_half", tag=tag, align_bytes=ALIGN)
+            y_half[g] = held.tile([P, (end - first) * C], F32, name="y_half", tag=tag, align_bytes=ALIGN)
             if g < RESULTS_ON_VECTOR:
-                nc.vector.tensor_scalar_mul(y_half[g][:], y[g][:], 0.5)
+                nc.vector.tensor_scalar_mul(y_half[g][:], y[:], 0.5)
             else:
-                nc.scalar.activation(y_half[g][:], y[g][:], ACT.Copy, scale=0.5)
+                nc.scalar.activation(y_half[g][:], y[:], ACT.Copy, scale=0.5)
 
         def scatter(g):
-            first, end = PAIR * g, PAIR * (g + 1)
+            first, end = groups[g]
             piece, place = locate(gate_cuts, first)
             nc.vector.tensor_tensor(
-                combined[:].indirect(offsets[:, first * LIST_COLS : end * LIST_COLS]),
+                combined[:].indirect(list_slice(first, end)),
                 y_half[g][:],
-                gate_sb[piece][:, place * C : (place + PAIR) * C],
+                gate_sb[piece][:, place * C : (place + end - first) * C],
                 ALU.mult,
             )
 
         def output_gate(half, tag):
             cols = slice(half * BANK, (half + 1) * BANK)
-            gate_pre = psum.tile([P, BANK], F32, name="gate_pre", tag=f"first{2 * half}")
+            gate_pre = psum.tile([P, BANK], F32, name="gate_pre", tag=GATE_BANK[half])
             nc.tensor.matmul_mx(
                 out=gate_pre[:],
                 lhsT=wg_w[:].bitcast(FP4X4),
@@ -233,36 +233,56 @@ def tile_moe_ogt_silu_sigmoid_kernel(
             gate_tanh[half] = held.tile([P, BANK], F32, name="gate_tanh", tag=tag, align_bytes=ALIGN)
             nc.scalar.activation(gate_tanh[half][:], gate_pre[:], ACT.Tanh, bias=zero_bias[:], scale=0.5)
 
-        warm = psum.tile([P, BANK], F32, name="warm", tag=RESULT_BANK[0])
-        for i in range(WARM_PASSES):
-            nc.tensor.matmul_mx(
-                out=warm[:],
-                lhsT=wg_w[:].bitcast(FP4X4),
-                lhsT_scale=x_plane[:, 0:N],
-                rhs=x_w[:, 0:BANK].bitcast(FP8X4),
-                rhs_scale=x_plane[:, 0:BANK],
-                start=True,
-                stop=True,
-            )
+        warm = psum.tile([P, BANK], F32, name="warm", tag="c")
+        nc.tensor.matmul_mx(
+            out=warm[:],
+            lhsT=wg_w[:].bitcast(FP4X4),
+            lhsT_scale=x_plane[:, 0:N],
+            rhs=x_w[:, 0:BANK].bitcast(FP8X4),
+            rhs_scale=x_plane[:, 0:BANK],
+            start=True,
+            stop=True,
+        )
+        gather_bytes(0, "slot_plane0")
+        for piece in range(len(WORD_GATHERS) - 1):
+            gather_words(piece, f"slot_words{piece}")
+        first_layer(0)
+        first_layer(1)
+        gather_bytes(1, "slot_words0")
+        gather_words(len(WORD_GATHERS) - 1, "slot_words1")
+        first_layer(2)
+        turn(0)
+        lay_out(0)
+        first_layer(3)
+        turn(1)
+        lay_out(1)
+        quantise(0, "h_codes0")
+        first_layer(4)
+        turn(2)
+        lay_out(2)
+        first_layer(5)
+        turn(3)
+        lay_out(3)
+        second_layer(0, "y_half0")
+        quantise(1, "h_codes0")
+        scatter(0)
+        first_layer(6)
+        first_layer(7)
+        turn(4)
+        lay_out(4)
+        second_layer(1, "h_couples5")
+        quantise(2, "h_codes2")
+        scatter(1)
+        turn(5)
+        lay_out(5)
+        second_layer(2, "h_couples7")
+        quantise(3, "h_codes3")
+        scatter(2)
+        second_layer(3, "y_half3")
+        scatter(3)
 
-        for e in range(FIRST_AHEAD):
-            first_layer(e)
-        for g in range(PAIRS):
-            for e in range(PAIR * g, PAIR * (g + 1)):
-                if e + FIRST_AHEAD < E:
-                    first_layer(e + FIRST_AHEAD)
-                turn(e)
-            lay_out(g)
-            if g > 0:
-                second_layer(g - 1)
-            quantise(g)
-            if g > 0:
-                scatter(g - 1)
-        second_layer(PAIRS - 1)
-        scatter(PAIRS - 1)
-
-        output_gate(0, f"h_codes{PAIRS - 1}")
-        output_gate(1, f"h_plane{PAIRS - 1}")
+        output_gate(0, "h_codes3")
+        output_gate(1, "h_plane3")
 
         for first in range(0, T, OUT_COLS):
             half, at = divmod(first, BANK)

@@ -78,7 +78,6 @@ def tile_moe_ogt_silu_sigmoid_kernel(
 
         nc.gpsimd.memset(zero_src[:], 0.0)
         nc.scalar.activation(zero_bias[:], zero_src[:], ACT.Silu)
-        nc.gpsimd.dma_start(wg_w[:].bitcast(I32), wg_words[0].bitcast(I32))
         make_identity(nc, ident[:])
 
         def load_token_plane():
@@ -111,6 +110,7 @@ def tile_moe_ogt_silu_sigmoid_kernel(
         nc.sync.dma_start(offsets[:], offs)
         load_token_plane()
         nc.sync.dma_start(x_w[:].bitcast(I32), x_words.rearrange("s p t d -> p (s t d)").bitcast(I32))
+        nc.sync.dma_start(wg_w[:].bitcast(I32), wg_words[0].bitcast(I32))
         load_w1(0)
         load_expert_planes(w1_plane, w1_scales)
         for piece in range(1, len(W1_LOADS) - 1):

@@ -22,8 +22,9 @@ BANK = 512
 ALIGN = 64
 LIST_COLS = C // 16
 
-W1_LOADS = (1, 2, 3, 2)
+W1_LOADS = (1, 2, 1, 2, 2)
 GATE_LOADS = (2, 6)
+W2_LOADS = (4, 4)
 BYTE_GATHERS = (4, 4)
 WORD_GATHERS = (1, 1, 2, 2, 2)
 GROUPS = (2, 2, 2, 2)
@@ -35,6 +36,7 @@ TURN_BANK = ("a", "d", "b", "a", "c", "a")
 RESULT_BANK = ("c", "d", "b", "c")
 GATE_BANK = ("first0", "first2")
 OUT_COLS = 256
+WARM_PASSES = 2
 
 
 def ranges(sizes):
@@ -52,7 +54,7 @@ def tile_moe_ogt_silu_sigmoid_kernel(
 ):
     nc = tc.nc
     w1_cuts, gate_cuts = ranges(W1_LOADS), ranges(GATE_LOADS)
-    groups, turns = ranges(GROUPS), ranges(TURNS)
+    groups, turns, w2_cuts = ranges(GROUPS), ranges(TURNS), ranges(W2_LOADS)
     byte_cuts, word_cuts = ranges(BYTE_GATHERS), ranges(WORD_GATHERS)
 
     with ExitStack() as ctx:
@@ -72,7 +74,9 @@ def tile_moe_ogt_silu_sigmoid_kernel(
         w1_w = [
             held.tile([P, end - first, 2 * H], U8, name=f"w1_w{first}", align_bytes=ALIGN) for first, end in w1_cuts
         ]
-        w2_w = held.tile([P, E, 2 * N], U8, name="w2_w", align_bytes=ALIGN)
+        w2_w = [
+            held.tile([P, end - first, 2 * N], U8, name=f"w2_w{first}", align_bytes=ALIGN) for first, end in w2_cuts
+        ]
         gate_sb = [held.tile([P, (end - first) * C], F32, name=f"gate{first}") for first, end in gate_cuts]
         wg_w = held.tile([P, 2 * N], U8, name="wg_w", align_bytes=ALIGN)
 
@@ -103,6 +107,12 @@ def tile_moe_ogt_silu_sigmoid_kernel(
                 w1_w[piece][:].bitcast(I32), w1_words.bitcast(I32)[first:end, 0].rearrange("e p w -> p e w")
             )
 
+        def load_w2(piece):
+            first, end = w2_cuts[piece]
+            nc.sync.dma_start(
+                w2_w[piece][:].bitcast(I32), w2_words.bitcast(I32)[first:end, 0].rearrange("e p w -> p e w")
+            )
+
         def load_gate(piece):
             first, end = gate_cuts[piece]
             nc.sync.dma_start(gate_sb[piece][:], gate[:, first * C : end * C])
@@ -116,9 +126,10 @@ def tile_moe_ogt_silu_sigmoid_kernel(
         for piece in range(1, len(W1_LOADS) - 1):
             load_w1(piece)
         load_expert_planes(w2_plane, w2_scales)
-        nc.sync.dma_start(w2_w[:].bitcast(I32), w2_words.rearrange("e s p w -> p (e s) w").bitcast(I32))
+        load_w2(0)
         load_w1(len(W1_LOADS) - 1)
         load_gate(0)
+        load_w2(1)
         load_gate(1)
         load_gate_plane()
 
@@ -193,9 +204,10 @@ def tile_moe_ogt_silu_sigmoid_kernel(
             y = psum.tile([P, (end - first) * C], F32, name="y", tag=RESULT_BANK[g])
             for e in range(first, end):
                 cols = slice((e - first) * C, (e - first + 1) * C)
+                w2_piece, w2_place = locate(w2_cuts, e)
                 nc.tensor.matmul_mx(
                     out=y[:, cols],
-                    lhsT=w2_w[:, e, :].bitcast(FP4X4),
+                    lhsT=w2_w[w2_piece][:, w2_place, :].bitcast(FP4X4),
                     lhsT_scale=w2_plane[:, e, :],
                     rhs=h_codes[g][:, cols].bitcast(FP8X4),
                     rhs_scale=h_planes[g][:, cols],
@@ -234,15 +246,16 @@ def tile_moe_ogt_silu_sigmoid_kernel(
             nc.scalar.activation(gate_tanh[half][:], gate_pre[:], ACT.Tanh, bias=zero_bias[:], scale=0.5)
 
         warm = psum.tile([P, BANK], F32, name="warm", tag="c")
-        nc.tensor.matmul_mx(
-            out=warm[:],
-            lhsT=wg_w[:].bitcast(FP4X4),
-            lhsT_scale=x_plane[:, 0:N],
-            rhs=x_w[:, 0:BANK].bitcast(FP8X4),
-            rhs_scale=x_plane[:, 0:BANK],
-            start=True,
-            stop=True,
-        )
+        for i in range(WARM_PASSES):
+            nc.tensor.matmul_mx(
+                out=warm[:],
+                lhsT=wg_w[:].bitcast(FP4X4),
+                lhsT_scale=x_plane[:, 0:N],
+                rhs=x_w[:, 0:BANK].bitcast(FP8X4),
+                rhs_scale=x_plane[:, 0:BANK],
+                start=True,
+                stop=True,
+            )
         gather_bytes(0, "slot_plane0")
         for piece in range(len(WORD_GATHERS) - 1):
             gather_words(piece, f"slot_words{piece}")

@@ -23,6 +23,7 @@ ALIGN = 64
 LIST_COLS = C // 16
 
 W1_LOADS = (1, 2, 1, 2, 2)
+W1_PLANES = (4, 4)
 GATE_LOADS = (2, 6)
 W2_LOADS = (4, 4)
 BYTE_GATHERS = (4, 4)
@@ -55,6 +56,7 @@ def tile_moe_ogt_silu_sigmoid_kernel(
     nc = tc.nc
     w1_cuts, gate_cuts = ranges(W1_LOADS), ranges(GATE_LOADS)
     groups, turns, w2_cuts = ranges(GROUPS), ranges(TURNS), ranges(W2_LOADS)
+    plane_cuts = ranges(W1_PLANES)
     byte_cuts, word_cuts = ranges(BYTE_GATHERS), ranges(WORD_GATHERS)
 
     with ExitStack() as ctx:
@@ -64,7 +66,9 @@ def tile_moe_ogt_silu_sigmoid_kernel(
         offsets = held.tile([P, T // 16], U16, name="offsets")
         x_w = held.tile([P, T], U32, name="x_w", align_bytes=ALIGN)
         x_plane = held.tile([P, T], U8, name="x_plane", align_bytes=ALIGN)
-        w1_plane = held.tile([P, E, H], U8, name="w1_plane", align_bytes=ALIGN)
+        w1_planes = [
+            held.tile([P, end - first, H], U8, name=f"w1_plane{first}", align_bytes=ALIGN) for first, end in plane_cuts
+        ]
         w2_plane = held.tile([P, E, N], U8, name="w2_plane", align_bytes=ALIGN)
         wg_plane = held.tile([P, N], U8, name="wg_plane", align_bytes=ALIGN)
         ident = held.tile([P, P], F32, name="ident")
@@ -122,9 +126,11 @@ def tile_moe_ogt_silu_sigmoid_kernel(
         nc.sync.dma_start(x_w[:].bitcast(I32), x_words.rearrange("s p t d -> p (s t d)").bitcast(I32))
         nc.sync.dma_start(wg_w[:].bitcast(I32), wg_words[0].bitcast(I32))
         load_w1(0)
-        load_expert_planes(w1_plane, w1_scales)
-        for piece in range(1, len(W1_LOADS) - 1):
-            load_w1(piece)
+        load_expert_planes(w1_planes[0], w1_scales[: W1_PLANES[0]])
+        load_w1(1)
+        load_w1(2)
+        load_expert_planes(w1_planes[1], w1_scales[W1_PLANES[0] :])
+        load_w1(3)
         load_expert_planes(w2_plane, w2_scales)
         load_w2(0)
         load_w1(len(W1_LOADS) - 1)
@@ -154,6 +160,7 @@ def tile_moe_ogt_silu_sigmoid_kernel(
             w1_piece, w1_place = locate(w1_cuts, e)
             word_piece, word_place = locate(word_cuts, e)
             byte_piece, byte_place = locate(byte_cuts, e)
+            plane_piece, plane_place = locate(plane_cuts, e)
             bank = e if e < FIRST_BANKS else 1 + (e - 1) % (FIRST_BANKS - 1)
             pre = psum.tile([P, H], F32, name="pre", tag=f"first{bank}")
             nc.tensor.matmul_mx(
@@ -161,7 +168,7 @@ def tile_moe_ogt_silu_sigmoid_kernel(
                 lhsT=slot_words[word_piece][:, word_place * C : (word_place + 1) * C].bitcast(FP8X4),
                 lhsT_scale=slot_planes[byte_piece][:, byte_place * C : (byte_place + 1) * C],
                 rhs=w1_w[w1_piece][:, w1_place, :].bitcast(FP4X4),
-                rhs_scale=w1_plane[:, e, :],
+                rhs_scale=w1_planes[plane_piece][:, plane_place, :],
                 start=True,
                 stop=True,
             )

@@ -23,7 +23,7 @@ ALIGN = 64
 LIST_COLS = C // 16
 
 W1_LOADS = (1, 2, 1, 2, 2)
-W1_PLANES = (4, 4)
+W1_PLANES = (6, 2)
 GATE_LOADS = (2, 6)
 W2_LOADS = (4, 4)
 BYTE_GATHERS = (4, 4)
@@ -129,8 +129,8 @@ def tile_moe_ogt_silu_sigmoid_kernel(
         load_expert_planes(w1_planes[0], w1_scales[: W1_PLANES[0]])
         load_w1(1)
         load_w1(2)
-        load_expert_planes(w1_planes[1], w1_scales[W1_PLANES[0] :])
         load_w1(3)
+        load_expert_planes(w1_planes[1], w1_scales[W1_PLANES[0] :])
         load_expert_planes(w2_plane, w2_scales)
         load_w2(0)
         load_w1(len(W1_LOADS) - 1)

@@ -24,7 +24,7 @@ LIST_COLS = C // 16
 
 W1_LOADS = (1, 2, 1, 2, 2)
 W1_PLANES = (6, 2)
-GATE_LOADS = (2, 6)
+GATE_LOADS = (4, 4)
 W2_LOADS = (4, 4)
 BYTE_GATHERS = (4, 4)
 WORD_GATHERS = (1, 1, 2, 2, 2)
@@ -32,12 +32,11 @@ GROUPS = (2, 2, 2, 2)
 TURNS = (1, 1, 1, 1, 2, 2)
 FIRST_BANKS = 4
 TURNS_ON_VECTOR = 4
-RESULTS_ON_VECTOR = 1
+LAST_ON_VECTOR = 320
 TURN_BANK = ("a", "d", "b", "a", "c", "a")
-RESULT_BANK = ("c", "d", "b", "c")
+RESULT_BANK = ("c", "d", "b", "first3")
 GATE_BANK = ("first0", "first2")
 OUT_COLS = 256
-WARM_PASSES = 2
 
 
 def ranges(sizes):
@@ -72,7 +71,8 @@ def tile_moe_ogt_silu_sigmoid_kernel(
         w2_plane = held.tile([P, E, N], U8, name="w2_plane", align_bytes=ALIGN)
         wg_plane = held.tile([P, N], U8, name="wg_plane", align_bytes=ALIGN)
         ident = held.tile([P, P], F32, name="ident")
-        combined = held.tile([P, T], F32, name="combined")
+        by_vector = held.tile([P, T], F32, name="by_vector")
+        by_scalar = held.tile([P, T], F32, name="by_scalar")
         zero_src = held.tile([P, 1], F32, name="zero_src")
         zero_bias = held.tile([P, 1], F32, name="zero_bias")
         w1_w = [
@@ -87,6 +87,8 @@ def tile_moe_ogt_silu_sigmoid_kernel(
         nc.gpsimd.memset(zero_src[:], 0.0)
         nc.scalar.activation(zero_bias[:], zero_src[:], ACT.Silu)
         make_identity(nc, ident[:])
+        nc.vector.memset(by_vector[:], 1.0)
+        nc.vector.memset(by_scalar[:], 1.0)
 
         def load_token_plane():
             rows = x_scales[0].bitcast(I32)
@@ -124,7 +126,6 @@ def tile_moe_ogt_silu_sigmoid_kernel(
         nc.sync.dma_start(offsets[:], offs)
         load_token_plane()
         nc.sync.dma_start(x_w[:].bitcast(I32), x_words.rearrange("s p t d -> p (s t d)").bitcast(I32))
-        nc.sync.dma_start(wg_w[:].bitcast(I32), wg_words[0].bitcast(I32))
         load_w1(0)
         load_expert_planes(w1_planes[0], w1_scales[: W1_PLANES[0]])
         load_w1(1)
@@ -136,12 +137,11 @@ def tile_moe_ogt_silu_sigmoid_kernel(
         load_w1(len(W1_LOADS) - 1)
         load_gate(0)
         load_w2(1)
-        load_gate(1)
+        nc.sync.dma_start(wg_w[:].bitcast(I32), wg_words[0].bitcast(I32))
         load_gate_plane()
+        load_gate(1)
 
-        slot_planes, slot_words, h_couples, turned, h_turned, h_codes, h_planes, y, y_half, gate_tanh = [
-            {} for i in range(10)
-        ]
+        slot_planes, slot_words, h_couples, turned, h_turned, h_codes, h_planes, y = [{} for i in range(8)]
 
         def list_slice(first, end):
             return offsets[:, first * LIST_COLS : end * LIST_COLS]
@@ -206,14 +206,14 @@ def tile_moe_ogt_silu_sigmoid_kernel(
             h_planes[g] = held.tile([P, (end - first) * C], U8, name="h_plane", tag=f"h_plane{g}", align_bytes=ALIGN)
             nc.vector.quantize_mx(out=h_codes[g][:].bitcast(FP8X4), scales=h_planes[g][:], in_=h_turned[g][:])
 
-        def second_layer(g, tag):
+        def second_layer(g):
             first, end = groups[g]
-            y = psum.tile([P, (end - first) * C], F32, name="y", tag=RESULT_BANK[g])
+            y[g] = psum.tile([P, (end - first) * C], F32, name="y", tag=RESULT_BANK[g])
             for e in range(first, end):
                 cols = slice((e - first) * C, (e - first + 1) * C)
                 w2_piece, w2_place = locate(w2_cuts, e)
                 nc.tensor.matmul_mx(
-                    out=y[:, cols],
+                    out=y[g][:, cols],
                     lhsT=w2_w[w2_piece][:, w2_place, :].bitcast(FP4X4),
                     lhsT_scale=w2_plane[:, e, :],
                     rhs=h_codes[g][:, cols].bitcast(FP8X4),
@@ -221,23 +221,18 @@ def tile_moe_ogt_silu_sigmoid_kernel(
                     start=True,
                     stop=True,
                 )
-            y_half[g] = held.tile([P, (end - first) * C], F32, name="y_half", tag=tag, align_bytes=ALIGN)
-            if g < RESULTS_ON_VECTOR:
-                nc.vector.tensor_scalar_mul(y_half[g][:], y[:], 0.5)
-            else:
-                nc.scalar.activation(y_half[g][:], y[:], ACT.Copy, scale=0.5)
 
-        def scatter(g):
+        def weigh(g, into):
             first, end = groups[g]
             piece, place = locate(gate_cuts, first)
-            nc.vector.tensor_tensor(
-                combined[:].indirect(list_slice(first, end)),
-                y_half[g][:],
-                gate_sb[piece][:, place * C : (place + end - first) * C],
-                ALU.mult,
+            nc.vector.scalar_tensor_tensor(
+                into, y[g][:], 0.5, gate_sb[piece][:, place * C : (place + end - first) * C], ALU.mult, ALU.mult
             )
 
-        def output_gate(half, tag):
+        def slots(first, end):
+            return offsets[:, first // 16 : end // 16]
+
+        def output_gate(half):
             cols = slice(half * BANK, (half + 1) * BANK)
             gate_pre = psum.tile([P, BANK], F32, name="gate_pre", tag=GATE_BANK[half])
             nc.tensor.matmul_mx(
@@ -249,20 +244,8 @@ def tile_moe_ogt_silu_sigmoid_kernel(
                 start=True,
                 stop=True,
             )
-            gate_tanh[half] = held.tile([P, BANK], F32, name="gate_tanh", tag=tag, align_bytes=ALIGN)
-            nc.scalar.activation(gate_tanh[half][:], gate_pre[:], ACT.Tanh, bias=zero_bias[:], scale=0.5)
+            nc.scalar.activation(gate_tanh[:, cols], gate_pre[:], ACT.Tanh, bias=zero_bias[:], scale=0.5)
 
-        warm = psum.tile([P, BANK], F32, name="warm", tag="c")
-        for i in range(WARM_PASSES):
-            nc.tensor.matmul_mx(
-                out=warm[:],
-                lhsT=wg_w[:].bitcast(FP4X4),
-                lhsT_scale=x_plane[:, 0:N],
-                rhs=x_w[:, 0:BANK].bitcast(FP8X4),
-                rhs_scale=x_plane[:, 0:BANK],
-                start=True,
-                stop=True,
-            )
         gather_bytes(0, "slot_plane0")
         for piece in range(len(WORD_GATHERS) - 1):
             gather_words(piece, f"slot_words{piece}")
@@ -283,32 +266,42 @@ def tile_moe_ogt_silu_sigmoid_kernel(
         first_layer(5)
         turn(3)
         lay_out(3)
-        second_layer(0, "y_half0")
+        pair = 2 * C
+        second_layer(0)
+        y_first = held.tile([P, pair], F32, name="y_first")
+        nc.vector.tensor_scalar_mul(y_first[:], y[0][:], 0.5)
         quantise(1, "h_codes0")
-        scatter(0)
+        nc.vector.tensor_tensor(by_vector[:].indirect(slots(0, pair)), y_first[:], gate_sb[0][:, :pair], ALU.mult)
         first_layer(6)
         first_layer(7)
         turn(4)
         lay_out(4)
-        second_layer(1, "h_couples5")
-        quantise(2, "h_codes2")
-        scatter(1)
+        second_layer(1)
         turn(5)
         lay_out(5)
-        second_layer(2, "h_couples7")
+        y_second = held.tile([P, pair], F32, name="y_second", tag="h_couples7", align_bytes=ALIGN)
+        weigh(1, y_second[:])
+        quantise(2, "h_codes2")
         quantise(3, "h_codes3")
-        scatter(2)
-        second_layer(3, "y_half3")
-        scatter(3)
+        nc.scalar.activation(by_scalar[:].indirect(slots(pair, 2 * pair)), y_second[:], ACT.Copy)
+        gate_tanh = held.tile([P, T], F32, name="gate_tanh", tag="h_couples7", align_bytes=ALIGN)
+        output_gate(0)
+        output_gate(1)
+        y_last = held.tile([P, 2 * pair], F32, name="y_last")
+        second_layer(2)
+        weigh(2, y_last[:, :pair])
+        second_layer(3)
+        weigh(3, y_last[:, pair:])
+        cut = 2 * pair + LAST_ON_VECTOR
+        nc.vector.tensor_copy(by_vector[:].indirect(slots(2 * pair, cut)), y_last[:, :LAST_ON_VECTOR])
+        nc.scalar.activation(by_scalar[:].indirect(slots(cut, T)), y_last[:, LAST_ON_VECTOR:], ACT.Copy)
 
-        output_gate(0, "h_codes3")
-        output_gate(1, "h_plane3")
-
+        part = held.tile([P, T], F32, name="part")
+        for half in range(2):
+            cols = slice(half * BANK, (half + 1) * BANK)
+            nc.vector.scalar_tensor_tensor(part[:, cols], gate_tanh[:, cols], 1.0, by_vector[:, cols], ALU.add, ALU.mult)
         for first in range(0, T, OUT_COLS):
-            half, at = divmod(first, BANK)
             cols = slice(first, first + OUT_COLS)
             result = held.tile([P, OUT_COLS], F32, name=f"result{first}")
-            nc.vector.scalar_tensor_tensor(
-                result[:], gate_tanh[half][:, at : at + OUT_COLS], 1.0, combined[:, cols], ALU.add, ALU.mult
-            )
+            nc.vector.tensor_tensor(result[:], part[:, cols], by_scalar[:, cols], ALU.mult)
             nc.sync.dma_start(out[:, cols], result[:])

@@ -20,23 +20,15 @@ ALU = mybir.AluOpType
 
 BANK = 512
 ALIGN = 64
-LIST_COLS = C // 16
-
-W1_LOADS = (1, 2, 1, 2, 2)
-W1_PLANES = (6, 2)
-GATE_LOADS = (4, 4)
+PAIR = 2 * C
+W1_LOADS = (1, 3, 2, 2)
+W1_PLANES = (8,)
 W2_LOADS = (4, 4)
+GATE_LOADS = (4, 4)
 BYTE_GATHERS = (4, 4)
 WORD_GATHERS = (1, 1, 2, 2, 2)
-GROUPS = (2, 2, 2, 2)
-TURNS = (1, 1, 1, 1, 2, 2)
-FIRST_BANKS = 4
-TURNS_ON_VECTOR = 4
-LAST_ON_VECTOR = 320
-TURN_BANK = ("a", "d", "b", "a", "c", "a")
-RESULT_BANK = ("c", "d", "b", "first3")
-GATE_BANK = ("first0", "first2")
-OUT_COLS = 256
+PART_COLS = (512, 512)
+OUT_COLS = (256, 256, 256, 256)
 
 
 def ranges(sizes):
@@ -53,36 +45,33 @@ def tile_moe_ogt_silu_sigmoid_kernel(
     tc, x_words, x_scales, wg_words, wg_scales, w1_words, w1_scales, w2_words, w2_scales, gate, offs, out
 ):
     nc = tc.nc
-    w1_cuts, gate_cuts = ranges(W1_LOADS), ranges(GATE_LOADS)
-    groups, turns, w2_cuts = ranges(GROUPS), ranges(TURNS), ranges(W2_LOADS)
-    plane_cuts = ranges(W1_PLANES)
+    w1_cuts, plane_cuts, w2_cuts, gate_cuts = ranges(W1_LOADS), ranges(W1_PLANES), ranges(W2_LOADS), ranges(GATE_LOADS)
     byte_cuts, word_cuts = ranges(BYTE_GATHERS), ranges(WORD_GATHERS)
 
     with ExitStack() as ctx:
         held = ctx.enter_context(tc.tile_pool(name="held", bufs=1))
         psum = ctx.enter_context(tc.psum_pool(name="psum", bufs=1))
 
+        def sbuf(shape, dtype, name, tag=None):
+            return held.tile(shape, dtype, name=name, tag=tag or name, align_bytes=ALIGN)
+
         offsets = held.tile([P, T // 16], U16, name="offsets")
-        x_w = held.tile([P, T], U32, name="x_w", align_bytes=ALIGN)
-        x_plane = held.tile([P, T], U8, name="x_plane", align_bytes=ALIGN)
-        w1_planes = [
-            held.tile([P, end - first, H], U8, name=f"w1_plane{first}", align_bytes=ALIGN) for first, end in plane_cuts
-        ]
-        w2_plane = held.tile([P, E, N], U8, name="w2_plane", align_bytes=ALIGN)
-        wg_plane = held.tile([P, N], U8, name="wg_plane", align_bytes=ALIGN)
-        ident = held.tile([P, P], F32, name="ident")
-        by_vector = held.tile([P, T], F32, name="by_vector")
-        by_scalar = held.tile([P, T], F32, name="by_scalar")
-        zero_src = held.tile([P, 1], F32, name="zero_src")
-        zero_bias = held.tile([P, 1], F32, name="zero_bias")
-        w1_w = [
-            held.tile([P, end - first, 2 * H], U8, name=f"w1_w{first}", align_bytes=ALIGN) for first, end in w1_cuts
-        ]
-        w2_w = [
-            held.tile([P, end - first, 2 * N], U8, name=f"w2_w{first}", align_bytes=ALIGN) for first, end in w2_cuts
-        ]
-        gate_sb = [held.tile([P, (end - first) * C], F32, name=f"gate{first}") for first, end in gate_cuts]
-        wg_w = held.tile([P, 2 * N], U8, name="wg_w", align_bytes=ALIGN)
+        x_w = sbuf([P, T], U32, "x_w")
+        x_plane = sbuf([P, T], U8, "x_plane")
+        w1_w = [sbuf([P, end - first, 2 * H], U8, f"w1_w{first}") for first, end in w1_cuts]
+        w1_planes = [sbuf([P, end - first, H], U8, f"w1_plane{first}") for first, end in plane_cuts]
+        w2_w = [sbuf([P, end - first, 2 * N], U8, f"w2_w{first}") for first, end in w2_cuts]
+        w2_plane = sbuf([P, E, N], U8, "w2_plane")
+        wg_w = sbuf([P, 2 * N], U8, "wg_w")
+        wg_plane = sbuf([P, 1, N], U8, "wg_plane")
+        gate_sb = [sbuf([P, (end - first) * C], F32, f"gate{first}") for first, end in gate_cuts]
+        ident = sbuf([P, P], F32, "ident")
+        by_vector = sbuf([P, T], F32, "by_vector")
+        by_scalar = sbuf([P, T], F32, "by_scalar")
+        gate_tanh = sbuf([P, T], F32, "gate_tanh")
+        weighed = sbuf([P, T], F32, "weighed")
+        zero_src = sbuf([P, 1], F32, "zero_src")
+        zero_bias = sbuf([P, 1], F32, "zero_bias")
 
         nc.gpsimd.memset(zero_src[:], 0.0)
         nc.scalar.activation(zero_bias[:], zero_src[:], ACT.Silu)
@@ -90,79 +79,68 @@ def tile_moe_ogt_silu_sigmoid_kernel(
         nc.vector.memset(by_vector[:], 1.0)
         nc.vector.memset(by_scalar[:], 1.0)
 
-        def load_token_plane():
+        def load_token_plane(q):
             rows = x_scales[0].bitcast(I32)
-            for q in range(4):
-                nc.sync.dma_start(
-                    x_plane[32 * q : 32 * (q + 1), :].bitcast(I32), rows[4 * q : 4 * (q + 1), :].partition_broadcast(8)
-                )
+            nc.sync.dma_start(
+                x_plane[32 * q : 32 * (q + 1), :].bitcast(I32), rows[4 * q : 4 * (q + 1), :].partition_broadcast(8)
+            )
 
-        def load_gate_plane():
-            rows = wg_scales[0].rearrange("(q r) w -> r q w", r=4)
-            for r in range(4):
-                nc.sync.dma_start(wg_plane[r:P:32, :].bitcast(I32), rows[r].bitcast(I32))
+        def load_rows(plane, scales, r):
+            rows = scales.rearrange("e (q r) w -> r q e w", r=4)
+            nc.sync.dma_start(plane[r:P:32, :, :].bitcast(I32), rows[r].bitcast(I32))
 
-        def load_expert_planes(plane, scales):
-            rows = scales.rearrange("e s (q r) w -> r q (e s) w", r=4)
-            for r in range(4):
-                nc.sync.dma_start(plane[r:P:32, :, :].bitcast(I32), rows[r].bitcast(I32))
+        def load_w1_rows(piece, r):
+            first, end = plane_cuts[piece]
+            load_rows(w1_planes[piece], w1_scales[first:end, 0], r)
+
+        def load_w2_rows(r):
+            load_rows(w2_plane, w2_scales[:, 0], r)
+
+        def load_wg_rows(r):
+            load_rows(wg_plane, wg_scales, r)
+
+        def load_words(tile, words):
+            nc.sync.dma_start(tile[:].bitcast(I32), words.bitcast(I32).rearrange("e p w -> p e w"))
 
         def load_w1(piece):
             first, end = w1_cuts[piece]
-            nc.sync.dma_start(
-                w1_w[piece][:].bitcast(I32), w1_words.bitcast(I32)[first:end, 0].rearrange("e p w -> p e w")
-            )
+            load_words(w1_w[piece], w1_words[first:end, 0])
 
         def load_w2(piece):
             first, end = w2_cuts[piece]
-            nc.sync.dma_start(
-                w2_w[piece][:].bitcast(I32), w2_words.bitcast(I32)[first:end, 0].rearrange("e p w -> p e w")
-            )
+            load_words(w2_w[piece], w2_words[first:end, 0])
+
+        def load_wg():
+            nc.sync.dma_start(wg_w[:].bitcast(I32), wg_words[0].bitcast(I32))
+
+        def load_x():
+            nc.sync.dma_start(x_w[:].bitcast(I32), x_words.rearrange("s p t d -> p (s t d)").bitcast(I32))
 
         def load_gate(piece):
             first, end = gate_cuts[piece]
             nc.sync.dma_start(gate_sb[piece][:], gate[:, first * C : end * C])
 
-        nc.sync.dma_start(offsets[:], offs)
-        load_token_plane()
-        nc.sync.dma_start(x_w[:].bitcast(I32), x_words.rearrange("s p t d -> p (s t d)").bitcast(I32))
-        load_w1(0)
-        load_expert_planes(w1_planes[0], w1_scales[: W1_PLANES[0]])
-        load_w1(1)
-        load_w1(2)
-        load_w1(3)
-        load_expert_planes(w1_planes[1], w1_scales[W1_PLANES[0] :])
-        load_expert_planes(w2_plane, w2_scales)
-        load_w2(0)
-        load_w1(len(W1_LOADS) - 1)
-        load_gate(0)
-        load_w2(1)
-        nc.sync.dma_start(wg_w[:].bitcast(I32), wg_words[0].bitcast(I32))
-        load_gate_plane()
-        load_gate(1)
-
         slot_planes, slot_words, h_couples, turned, h_turned, h_codes, h_planes, y = [{} for i in range(8)]
 
-        def list_slice(first, end):
-            return offsets[:, first * LIST_COLS : end * LIST_COLS]
+        def slots(first, end):
+            return offsets[:, first // 16 : end // 16]
 
-        def gather_bytes(piece, tag):
+        def gather_bytes(piece, tag=None):
             first, end = byte_cuts[piece]
-            slot_planes[piece] = held.tile([P, (end - first) * C], U8, name="slot_plane", tag=tag, align_bytes=ALIGN)
-            nc.vector.tensor_copy(slot_planes[piece][:], x_plane[:].indirect(list_slice(first, end)))
+            slot_planes[piece] = sbuf([P, (end - first) * C], U8, f"slot_plane{piece}", tag)
+            nc.vector.tensor_copy(slot_planes[piece][:], x_plane[:].indirect(slots(first * C, end * C)))
 
-        def gather_words(piece, tag):
+        def gather_words(piece, tag=None):
             first, end = word_cuts[piece]
-            slot_words[piece] = held.tile([P, (end - first) * C], U32, name="slot_words", tag=tag, align_bytes=ALIGN)
-            nc.vector.tensor_copy(slot_words[piece][:], x_w[:].indirect(list_slice(first, end)))
+            slot_words[piece] = sbuf([P, (end - first) * C], U32, f"slot_words{piece}", tag)
+            nc.vector.tensor_copy(slot_words[piece][:], x_w[:].indirect(slots(first * C, end * C)))
 
-        def first_layer(e):
+        def first_layer(e, bank, tag=None):
             w1_piece, w1_place = locate(w1_cuts, e)
             word_piece, word_place = locate(word_cuts, e)
             byte_piece, byte_place = locate(byte_cuts, e)
             plane_piece, plane_place = locate(plane_cuts, e)
-            bank = e if e < FIRST_BANKS else 1 + (e - 1) % (FIRST_BANKS - 1)
-            pre = psum.tile([P, H], F32, name="pre", tag=f"first{bank}")
+            pre = psum.tile([P, H], F32, name="pre", tag=bank)
             nc.tensor.matmul_mx(
                 out=pre[:],
                 lhsT=slot_words[word_piece][:, word_place * C : (word_place + 1) * C].bitcast(FP8X4),
@@ -172,45 +150,35 @@ def tile_moe_ogt_silu_sigmoid_kernel(
                 start=True,
                 stop=True,
             )
-            h_couples[e] = held.tile([P, 2, P, 2], BF16, name="h_couples", tag=f"h_couples{e}", align_bytes=ALIGN)
+            h_couples[e] = sbuf([P, 2, P, 2], BF16, f"h_couples{e}", tag)
             nc.scalar.activation(
                 h_couples[e][:], pre[:].rearrange("s (p u d) -> s u p d", u=2, d=2), ACT.Silu, bias=zero_bias[:]
             )
 
-        def turn(g):
-            first, end = turns[g]
-            size = end - first
-            turned[g] = psum.tile([P, size, 2, C], F32, name="turned", tag=TURN_BANK[g])
-            for e in range(first, end):
-                words = h_couples[e][:].rearrange("s u p d -> s (u p d)").bitcast(F32)
+        def turn(g, bank):
+            turned[g] = psum.tile([P, 2, 2, C], F32, name="turned", tag=bank)
+            for place in range(2):
+                words = h_couples[2 * g + place][:].rearrange("s u p d -> s (u p d)").bitcast(F32)
                 for u in range(2):
-                    nc.tensor.transpose(turned[g][:, e - first, u, :], words[:, u * P : (u + 1) * P], ident[:])
+                    nc.tensor.transpose(turned[g][:, place, u, :], words[:, u * P : (u + 1) * P], ident[:])
 
-        def lay_out(g):
-            first, end = turns[g]
-            group, place = locate(groups, first)
-            if place == 0:
-                h_turned[group] = held.tile(
-                    [P, GROUPS[group] * H], BF16, name="h_turned", tag=f"h_turned{group}", align_bytes=ALIGN
-                )
-            laid = h_turned[group][:, place * H : (place + end - first) * H]
-            move = nc.vector.tensor_copy if g < TURNS_ON_VECTOR else nc.scalar.copy
+        def lay_out(g, tag=None, move=nc.vector.tensor_copy):
+            h_turned[g] = sbuf([P, 2 * H], BF16, f"h_turned{g}", tag)
             move(
-                laid.bitcast(F32).rearrange("p (e s u) -> p e s u", s=C, u=2),
+                h_turned[g][:].bitcast(F32).rearrange("p (e s u) -> p e s u", s=C, u=2),
                 turned[g][:].rearrange("p e u s -> p e s u"),
             )
 
-        def quantise(g, tag):
-            first, end = groups[g]
-            h_codes[g] = held.tile([P, (end - first) * C], U32, name="h_codes", tag=tag, align_bytes=ALIGN)
-            h_planes[g] = held.tile([P, (end - first) * C], U8, name="h_plane", tag=f"h_plane{g}", align_bytes=ALIGN)
+        def quantise(g, tag=None, plane_tag=None):
+            h_codes[g] = sbuf([P, PAIR], U32, f"h_codes{g}", tag)
+            h_planes[g] = sbuf([P, PAIR], U8, f"h_plane{g}", plane_tag)
             nc.vector.quantize_mx(out=h_codes[g][:].bitcast(FP8X4), scales=h_planes[g][:], in_=h_turned[g][:])
 
-        def second_layer(g):
-            first, end = groups[g]
-            y[g] = psum.tile([P, (end - first) * C], F32, name="y", tag=RESULT_BANK[g])
-            for e in range(first, end):
-                cols = slice((e - first) * C, (e - first + 1) * C)
+        def second_layer(g, bank):
+            y[g] = psum.tile([P, PAIR], F32, name="y", tag=bank)
+            for place in range(2):
+                e = 2 * g + place
+                cols = slice(place * C, (place + 1) * C)
                 w2_piece, w2_place = locate(w2_cuts, e)
                 nc.tensor.matmul_mx(
                     out=y[g][:, cols],
@@ -222,23 +190,30 @@ def tile_moe_ogt_silu_sigmoid_kernel(
                     stop=True,
                 )
 
-        def weigh(g, into):
-            first, end = groups[g]
-            piece, place = locate(gate_cuts, first)
+        def weigh(g):
+            piece, place = locate(gate_cuts, 2 * g)
             nc.vector.scalar_tensor_tensor(
-                into, y[g][:], 0.5, gate_sb[piece][:, place * C : (place + end - first) * C], ALU.mult, ALU.mult
+                weighed[:, g * PAIR : (g + 1) * PAIR],
+                y[g][:],
+                0.5,
+                gate_sb[piece][:, place * C : place * C + PAIR],
+                ALU.mult,
+                ALU.mult,
             )
 
-        def slots(first, end):
-            return offsets[:, first // 16 : end // 16]
+        def scatter_vector(first, end):
+            nc.vector.tensor_copy(by_vector[:].indirect(slots(first, end)), weighed[:, first:end])
 
-        def output_gate(half):
+        def scatter_scalar(first, end):
+            nc.scalar.activation(by_scalar[:].indirect(slots(first, end)), weighed[:, first:end], ACT.Copy)
+
+        def output_gate(half, bank):
             cols = slice(half * BANK, (half + 1) * BANK)
-            gate_pre = psum.tile([P, BANK], F32, name="gate_pre", tag=GATE_BANK[half])
+            gate_pre = psum.tile([P, BANK], F32, name="gate_pre", tag=bank)
             nc.tensor.matmul_mx(
                 out=gate_pre[:],
                 lhsT=wg_w[:].bitcast(FP4X4),
-                lhsT_scale=wg_plane[:],
+                lhsT_scale=wg_plane[:, 0, :],
                 rhs=x_w[:, cols].bitcast(FP8X4),
                 rhs_scale=x_plane[:, cols],
                 start=True,
@@ -246,62 +221,76 @@ def tile_moe_ogt_silu_sigmoid_kernel(
             )
             nc.scalar.activation(gate_tanh[:, cols], gate_pre[:], ACT.Tanh, bias=zero_bias[:], scale=0.5)
 
-        gather_bytes(0, "slot_plane0")
-        for piece in range(len(WORD_GATHERS) - 1):
-            gather_words(piece, f"slot_words{piece}")
-        first_layer(0)
-        first_layer(1)
-        gather_bytes(1, "slot_words0")
-        gather_words(len(WORD_GATHERS) - 1, "slot_words1")
-        first_layer(2)
-        turn(0)
-        lay_out(0)
-        first_layer(3)
-        turn(1)
-        lay_out(1)
-        quantise(0, "h_codes0")
-        first_layer(4)
-        turn(2)
-        lay_out(2)
-        first_layer(5)
-        turn(3)
-        lay_out(3)
-        pair = 2 * C
-        second_layer(0)
-        y_first = held.tile([P, pair], F32, name="y_first")
-        nc.vector.tensor_scalar_mul(y_first[:], y[0][:], 0.5)
-        quantise(1, "h_codes0")
-        nc.vector.tensor_tensor(by_vector[:].indirect(slots(0, pair)), y_first[:], gate_sb[0][:, :pair], ALU.mult)
-        first_layer(6)
-        first_layer(7)
-        turn(4)
-        lay_out(4)
-        second_layer(1)
-        turn(5)
-        lay_out(5)
-        y_second = held.tile([P, pair], F32, name="y_second", tag="h_couples7", align_bytes=ALIGN)
-        weigh(1, y_second[:])
-        quantise(2, "h_codes2")
-        quantise(3, "h_codes3")
-        nc.scalar.activation(by_scalar[:].indirect(slots(pair, 2 * pair)), y_second[:], ACT.Copy)
-        gate_tanh = held.tile([P, T], F32, name="gate_tanh", tag="h_couples7", align_bytes=ALIGN)
-        output_gate(0)
-        output_gate(1)
-        y_last = held.tile([P, 2 * pair], F32, name="y_last")
-        second_layer(2)
-        weigh(2, y_last[:, :pair])
-        second_layer(3)
-        weigh(3, y_last[:, pair:])
-        cut = 2 * pair + LAST_ON_VECTOR
-        nc.vector.tensor_copy(by_vector[:].indirect(slots(2 * pair, cut)), y_last[:, :LAST_ON_VECTOR])
-        nc.scalar.activation(by_scalar[:].indirect(slots(cut, T)), y_last[:, LAST_ON_VECTOR:], ACT.Copy)
+        def finish():
+            part = sbuf([P, T], F32, "part")
+            for first, end in ranges(PART_COLS):
+                cols = slice(first, end)
+                nc.vector.scalar_tensor_tensor(part[:, cols], gate_tanh[:, cols], 1.0, by_vector[:, cols], ALU.add, ALU.mult)
+            for first, end in ranges(OUT_COLS):
+                result = sbuf([P, end - first], F32, f"result{first}")
+                nc.vector.tensor_tensor(result[:], part[:, first:end], by_scalar[:, first:end], ALU.mult)
+                nc.sync.dma_start(out[:, first:end], result[:])
 
-        part = held.tile([P, T], F32, name="part")
-        for half in range(2):
-            cols = slice(half * BANK, (half + 1) * BANK)
-            nc.vector.scalar_tensor_tensor(part[:, cols], gate_tanh[:, cols], 1.0, by_vector[:, cols], ALU.add, ALU.mult)
-        for first in range(0, T, OUT_COLS):
-            cols = slice(first, first + OUT_COLS)
-            result = held.tile([P, OUT_COLS], F32, name=f"result{first}")
-            nc.vector.tensor_tensor(result[:], part[:, cols], by_scalar[:, cols], ALU.mult)
-            nc.sync.dma_start(out[:, cols], result[:])
+        nc.sync.dma_start(offsets[:], offs)
+        for q in range(4):
+            load_token_plane(q)
+        load_x()
+        load_w1(0)
+        for r in range(3):
+            load_w1_rows(0, r)
+        load_w2_rows(0)
+        load_w1_rows(0, 3)
+        load_w1(1)
+        for r in range(1, 4):
+            load_w2_rows(r)
+        load_w1(2)
+        load_w1(3)
+        load_w2(0)
+        load_gate(0)
+        for r in range(4):
+            load_wg_rows(r)
+        load_wg()
+        load_gate(1)
+        load_w2(1)
+
+        gather_bytes(0)
+        for piece in range(4):
+            gather_words(piece)
+        first_layer(0, "a")
+        first_layer(1, "b")
+        gather_bytes(1, "slot_words0")
+        gather_words(4, "slot_words1")
+        first_layer(2, "c")
+        first_layer(3, "d")
+        turn(0, "e")
+        lay_out(0)
+        quantise(0)
+        first_layer(4, "a")
+        first_layer(5, "b")
+        turn(1, "f")
+        lay_out(1)
+        quantise(1)
+        first_layer(6, "c")
+        first_layer(7, "d")
+        second_layer(0, "g")
+        weigh(0)
+        scatter_scalar(0, 256)
+        turn(2, "e")
+        lay_out(2)
+        second_layer(1, "h")
+        weigh(1)
+        quantise(2)
+        scatter_scalar(256, 512)
+        turn(3, "f")
+        lay_out(3)
+        output_gate(0, "a")
+        output_gate(1, "b")
+        second_layer(2, "g")
+        weigh(2)
+        quantise(3, "h_codes2")
+        scatter_vector(512, 640)
+        second_layer(3, "h")
+        weigh(3)
+        scatter_vector(640, 800)
+        scatter_scalar(800, 1024)
+        finish()

@@ -21,8 +21,8 @@ ALU = mybir.AluOpType
 BANK = 512
 ALIGN = 64
 PAIR = 2 * C
-W1_LOADS = (1, 3, 2, 2)
-W1_PLANES = (8,)
+W1_LOADS = (1, 1, 2, 2, 2)
+W1_PLANES = (4, 4)
 W2_LOADS = (4, 4)
 GATE_LOADS = (4, 4)
 BYTE_GATHERS = (4, 4)
@@ -236,22 +236,23 @@ def tile_moe_ogt_silu_sigmoid_kernel(
             load_token_plane(q)
         load_x()
         load_w1(0)
-        for r in range(3):
+        for r in range(4):
             load_w1_rows(0, r)
-        load_w2_rows(0)
-        load_w1_rows(0, 3)
         load_w1(1)
-        for r in range(1, 4):
-            load_w2_rows(r)
         load_w1(2)
+        for r in range(4):
+            load_w1_rows(1, r)
         load_w1(3)
-        load_w2(0)
+        load_w1(4)
+        for r in range(4):
+            load_w2_rows(r)
         load_gate(0)
+        load_w2(0)
+        load_w2(1)
         for r in range(4):
             load_wg_rows(r)
         load_wg()
         load_gate(1)
-        load_w2(1)
 
         gather_bytes(0)
         for piece in range(4):
@@ -267,29 +268,29 @@ def tile_moe_ogt_silu_sigmoid_kernel(
         quantise(0)
         first_layer(4, "a")
         first_layer(5, "b")
-        turn(1, "f")
-        lay_out(1)
-        quantise(1)
         first_layer(6, "c")
         first_layer(7, "d")
+        turn(1, "a")
+        lay_out(1)
+        turn(2, "e")
+        lay_out(2, move=nc.scalar.copy)
         second_layer(0, "g")
         weigh(0)
+        quantise(1, "h_codes0")
+        quantise(2, None, "h_plane0")
         scatter_scalar(0, 256)
-        turn(2, "e")
-        lay_out(2)
+        turn(3, "g")
+        lay_out(3)
         second_layer(1, "h")
         weigh(1)
-        quantise(2)
         scatter_scalar(256, 512)
-        turn(3, "f")
-        lay_out(3)
-        output_gate(0, "a")
+        second_layer(2, "c")
+        output_gate(0, "f")
         output_gate(1, "b")
-        second_layer(2, "g")
         weigh(2)
-        quantise(3, "h_codes2")
+        quantise(3, "wg_w")
         scatter_vector(512, 640)
-        second_layer(3, "h")
+        second_layer(3, "d")
         weigh(3)
         scatter_vector(640, 800)
         scatter_scalar(800, 1024)

@@ -21,10 +21,10 @@ ALU = mybir.AluOpType
 BANK = 512
 ALIGN = 64
 PAIR = 2 * C
-W1_LOADS = (1, 1, 2, 2, 2)
+W1_LOADS = (1, 1, 2, 1, 1, 2)
 W1_PLANES = (4, 4)
-W2_LOADS = (4, 4)
-GATE_LOADS = (4, 4)
+W2_LOADS = (2, 6)
+GATE_LOADS = (2, 2, 4)
 BYTE_GATHERS = (4, 4)
 WORD_GATHERS = (1, 1, 2, 2, 2)
 PART_COLS = (512, 512)
@@ -74,14 +74,13 @@ def tile_moe_ogt_silu_sigmoid_kernel(
         zero_bias = sbuf([P, 1], F32, "zero_bias")
 
         nc.gpsimd.memset(zero_src[:], 0.0)
-        nc.scalar.activation(zero_bias[:], zero_src[:], ACT.Silu)
         make_identity(nc, ident[:])
         nc.vector.memset(by_vector[:], 1.0)
         nc.vector.memset(by_scalar[:], 1.0)
 
-        def load_token_plane(q):
+        def load_token_plane(q, queue):
             rows = x_scales[0].bitcast(I32)
-            nc.sync.dma_start(
+            queue.dma_start(
                 x_plane[32 * q : 32 * (q + 1), :].bitcast(I32), rows[4 * q : 4 * (q + 1), :].partition_broadcast(8)
             )
 
@@ -232,8 +231,11 @@ def tile_moe_ogt_silu_sigmoid_kernel(
                 nc.sync.dma_start(out[:, first:end], result[:])
 
         nc.sync.dma_start(offsets[:], offs)
-        for q in range(4):
-            load_token_plane(q)
+        load_token_plane(0, nc.sync)
+        load_token_plane(1, nc.sync)
+        load_token_plane(2, nc.scalar)
+        load_token_plane(3, nc.scalar)
+        nc.scalar.activation(zero_bias[:], zero_src[:], ACT.Silu)
         load_x()
         load_w1(0)
         for r in range(4):
@@ -244,15 +246,17 @@ def tile_moe_ogt_silu_sigmoid_kernel(
             load_w1_rows(1, r)
         load_w1(3)
         load_w1(4)
+        load_w1(5)
         for r in range(4):
             load_w2_rows(r)
         load_gate(0)
         load_w2(0)
         load_w2(1)
+        load_gate(1)
         for r in range(4):
             load_wg_rows(r)
         load_wg()
-        load_gate(1)
+        load_gate(2)
 
         gather_bytes(0)
         for piece in range(4):

@@ -173,8 +173,8 @@ def tile_moe_ogt_silu_sigmoid_kernel(
             h_planes[g] = sbuf([P, PAIR], U8, f"h_plane{g}", plane_tag)
             nc.vector.quantize_mx(out=h_codes[g][:].bitcast(FP8X4), scales=h_planes[g][:], in_=h_turned[g][:])
 
-        def second_layer(g, bank):
-            y[g] = psum.tile([P, PAIR], F32, name="y", tag=bank)
+        def second_layer(g, bank=None, into=None):
+            y[g] = into if bank is None else psum.tile([P, PAIR], F32, name="y", tag=bank)[:]
             for place in range(2):
                 e = 2 * g + place
                 cols = slice(place * C, (place + 1) * C)
@@ -193,7 +193,7 @@ def tile_moe_ogt_silu_sigmoid_kernel(
             piece, place = locate(gate_cuts, 2 * g)
             nc.vector.scalar_tensor_tensor(
                 weighed[:, g * PAIR : (g + 1) * PAIR],
-                y[g][:],
+                y[g],
                 0.5,
                 gate_sb[piece][:, place * C : place * C + PAIR],
                 ALU.mult,
@@ -206,11 +206,9 @@ def tile_moe_ogt_silu_sigmoid_kernel(
         def scatter_scalar(first, end):
             nc.scalar.activation(by_scalar[:].indirect(slots(first, end)), weighed[:, first:end], ACT.Copy)
 
-        def output_gate(half, bank):
-            cols = slice(half * BANK, (half + 1) * BANK)
-            gate_pre = psum.tile([P, BANK], F32, name="gate_pre", tag=bank)
+        def gate_product(cols, gate_pre):
             nc.tensor.matmul_mx(
-                out=gate_pre[:],
+                out=gate_pre,
                 lhsT=wg_w[:].bitcast(FP4X4),
                 lhsT_scale=wg_plane[:, 0, :],
                 rhs=x_w[:, cols].bitcast(FP8X4),
@@ -218,7 +216,14 @@ def tile_moe_ogt_silu_sigmoid_kernel(
                 start=True,
                 stop=True,
             )
-            nc.scalar.activation(gate_tanh[:, cols], gate_pre[:], ACT.Tanh, bias=zero_bias[:], scale=0.5)
+
+        def gate_function(cols, gate_pre):
+            nc.scalar.activation(gate_tanh[:, cols], gate_pre, ACT.Tanh, bias=zero_bias[:], scale=0.5)
+
+        def output_gate(first, end, bank):
+            gate_pre = psum.tile([P, end - first], F32, name="gate_pre", tag=bank)
+            gate_product(slice(first, end), gate_pre[:])
+            gate_function(slice(first, end), gate_pre[:])
 
         def finish():
             part = sbuf([P, T], F32, "part")
@@ -287,15 +292,18 @@ def tile_moe_ogt_silu_sigmoid_kernel(
         lay_out(3)
         second_layer(1, "h")
         weigh(1)
-        scatter_scalar(256, 512)
+        quantise(3)
+        scatter_scalar(256, 384)
+        scatter_vector(384, 512)
         second_layer(2, "c")
-        output_gate(0, "f")
-        output_gate(1, "b")
+        output_gate(0, 512, "f")
+        output_gate(512, 768, "b")
+        shared = psum.tile([P, 2, PAIR], F32, name="shared", tag="d")
+        gate_product(slice(768, T), shared[:, 0, :])
+        second_layer(3, into=shared[:, 1, :])
         weigh(2)
-        quantise(3, "wg_w")
-        scatter_vector(512, 640)
-        second_layer(3, "d")
         weigh(3)
-        scatter_vector(640, 800)
-        scatter_scalar(800, 1024)
+        gate_function(slice(768, T), shared[:, 0, :])
+        scatter_vector(512, 672)
+        scatter_scalar(672, 1024)
         finish()

@@ -28,7 +28,7 @@ GATE_LOADS = (2, 2, 4)
 BYTE_GATHERS = (4, 4)
 WORD_GATHERS = (1, 1, 2, 2, 2)
 PART_COLS = (512, 512)
-OUT_COLS = (256, 256, 256, 256)
+OUT_COLS = (128, 256, 256, 256, 128)
 
 
 def ranges(sizes):
@@ -304,6 +304,6 @@ def tile_moe_ogt_silu_sigmoid_kernel(
         weigh(2)
         weigh(3)
         gate_function(slice(768, T), shared[:, 0, :])
-        scatter_vector(512, 672)
-        scatter_scalar(672, 1024)
+        scatter_vector(512, 704)
+        scatter_scalar(704, 1024)
         finish()

@@ -25,7 +25,7 @@ W1_LOADS = (1, 1, 2, 1, 1, 2)
 W1_PLANES = (4, 4)
 W2_LOADS = (2, 6)
 GATE_LOADS = (2, 2, 4)
-BYTE_GATHERS = (4, 4)
+BYTE_GATHERS = (4, 2, 2)
 WORD_GATHERS = (1, 1, 2, 2, 2)
 PART_COLS = (512, 512)
 OUT_COLS = (128, 256, 256, 256, 128)
@@ -161,6 +161,59 @@ def tile_moe_ogt_silu_sigmoid_kernel(
                 for u in range(2):
                     nc.tensor.transpose(turned[g][:, place, u, :], words[:, u * P : (u + 1) * P], ident[:])
 
+        def turn_beside_gate(g, banks):
+            quarter = BANK // 2
+            both = [psum.tile([P, 2, quarter], F32, name="both", tag=bank) for bank in banks]
+            cols = [slice(BANK + place * quarter, BANK + (place + 1) * quarter) for place in range(2)]
+            for place in range(2):
+                gate_product(cols[place], both[place][:, 0, :])
+            for place in range(2):
+                words = h_couples[2 * g + place][:].rearrange("s u p d -> s (u p d)").bitcast(F32)
+                for u in range(2):
+                    nc.tensor.transpose(both[place][:, 1, u * C : (u + 1) * C], words[:, u * P : (u + 1) * P], ident[:])
+            h_turned[g] = sbuf([P, 2 * H], BF16, f"h_turned{g}")
+            for place in range(2):
+                nc.vector.tensor_copy(
+                    h_turned[g][:, place * H : (place + 1) * H].bitcast(F32).rearrange("p (s u) -> p s u", u=2),
+                    both[place][:, 1, :].rearrange("p (u s) -> p s u", u=2),
+                )
+                gate_function(cols[place], both[place][:, 0, :])
+
+        def first_layer_beside_turn(e, g, banks):
+            w1_piece, w1_place = locate(w1_cuts, e)
+            word_piece, word_place = locate(word_cuts, e)
+            byte_piece, byte_place = locate(byte_cuts, e)
+            plane_piece, plane_place = locate(plane_cuts, e)
+            half = H // 2
+            both = [psum.tile([P, 2, half], F32, name="both", tag=bank) for bank in banks]
+            for place in range(2):
+                nc.tensor.matmul_mx(
+                    out=both[place][:, 0, :],
+                    lhsT=slot_words[word_piece][:, word_place * C : (word_place + 1) * C].bitcast(FP8X4),
+                    lhsT_scale=slot_planes[byte_piece][:, byte_place * C : (byte_place + 1) * C],
+                    rhs=w1_w[w1_piece][:, w1_place, place * H : (place + 1) * H].bitcast(FP4X4),
+                    rhs_scale=w1_planes[plane_piece][:, plane_place, place * half : (place + 1) * half],
+                    start=True,
+                    stop=True,
+                )
+            for place in range(2):
+                words = h_couples[2 * g + place][:].rearrange("s u p d -> s (u p d)").bitcast(F32)
+                for u in range(2):
+                    nc.tensor.transpose(both[place][:, 1, u * C : (u + 1) * C], words[:, u * P : (u + 1) * P], ident[:])
+            h_couples[e] = sbuf([P, 2, P, 2], BF16, f"h_couples{e}")
+            h_turned[g] = sbuf([P, 2 * H], BF16, f"h_turned{g}")
+            for place in range(2):
+                nc.scalar.activation(
+                    h_couples[e][:, :, place * P // 2 : (place + 1) * P // 2, :],
+                    both[place][:, 0, :].rearrange("s (p u d) -> s u p d", u=2, d=2),
+                    ACT.Silu,
+                    bias=zero_bias[:],
+                )
+                nc.vector.tensor_copy(
+                    h_turned[g][:, place * H : (place + 1) * H].bitcast(F32).rearrange("p (s u) -> p s u", u=2),
+                    both[place][:, 1, :].rearrange("p (u s) -> p s u", u=2),
+                )
+
         def lay_out(g, tag=None, move=nc.vector.tensor_copy):
             h_turned[g] = sbuf([P, 2 * H], BF16, f"h_turned{g}", tag)
             move(
@@ -168,10 +221,15 @@ def tile_moe_ogt_silu_sigmoid_kernel(
                 turned[g][:].rearrange("p e u s -> p e s u"),
             )
 
-        def quantise(g, tag=None, plane_tag=None):
+        def quantise(g, tag=None, plane_tag=None, pieces=1):
             h_codes[g] = sbuf([P, PAIR], U32, f"h_codes{g}", tag)
             h_planes[g] = sbuf([P, PAIR], U8, f"h_plane{g}", plane_tag)
-            nc.vector.quantize_mx(out=h_codes[g][:].bitcast(FP8X4), scales=h_planes[g][:], in_=h_turned[g][:])
+            for first, end in ranges([PAIR // pieces] * pieces):
+                nc.vector.quantize_mx(
+                    out=h_codes[g][:, first:end].bitcast(FP8X4),
+                    scales=h_planes[g][:, first:end],
+                    in_=h_turned[g][:, 4 * first : 4 * end],
+                )
 
         def second_layer(g, bank=None, into=None):
             y[g] = into if bank is None else psum.tile([P, PAIR], F32, name="y", tag=bank)[:]
@@ -256,11 +314,11 @@ def tile_moe_ogt_silu_sigmoid_kernel(
             load_w2_rows(r)
         load_gate(0)
         load_w2(0)
-        load_w2(1)
-        load_gate(1)
         for r in range(4):
             load_wg_rows(r)
         load_wg()
+        load_w2(1)
+        load_gate(1)
         load_gate(2)
 
         gather_bytes(0)
@@ -269,41 +327,35 @@ def tile_moe_ogt_silu_sigmoid_kernel(
         first_layer(0, "a")
         first_layer(1, "b")
         gather_bytes(1, "slot_words0")
-        gather_words(4, "slot_words1")
+        gather_bytes(2, "slot_words1")
+        gather_words(4, "w1_w0")
         first_layer(2, "c")
         first_layer(3, "d")
-        turn(0, "e")
-        lay_out(0)
-        quantise(0)
-        first_layer(4, "a")
+        first_layer_beside_turn(4, 0, ("a", "e"))
+        quantise(0, pieces=2)
         first_layer(5, "b")
         first_layer(6, "c")
         first_layer(7, "d")
         turn(1, "a")
         lay_out(1)
-        turn(2, "e")
+        turn(2, "h")
         lay_out(2, move=nc.scalar.copy)
         second_layer(0, "g")
         weigh(0)
         quantise(1, "h_codes0")
         quantise(2, None, "h_plane0")
         scatter_scalar(0, 256)
-        turn(3, "g")
-        lay_out(3)
-        second_layer(1, "h")
+        output_gate(0, 512, "f")
+        turn_beside_gate(3, ("b", "c"))
+        second_layer(1, "e")
         weigh(1)
         quantise(3)
         scatter_scalar(256, 384)
         scatter_vector(384, 512)
-        second_layer(2, "c")
-        output_gate(0, 512, "f")
-        output_gate(512, 768, "b")
-        shared = psum.tile([P, 2, PAIR], F32, name="shared", tag="d")
-        gate_product(slice(768, T), shared[:, 0, :])
-        second_layer(3, into=shared[:, 1, :])
+        second_layer(2, "a")
+        second_layer(3, "d")
         weigh(2)
         weigh(3)
-        gate_function(slice(768, T), shared[:, 0, :])
         scatter_vector(512, 704)
         scatter_scalar(704, 1024)
         finish()

@@ -19,15 +19,18 @@ ACT = mybir.ActivationFunctionType
 ALU = mybir.AluOpType
 
 BANK = 512
+HALF_BANK = BANK // 2
 ALIGN = 64
 PAIR = 2 * C
+ROWS = 4
+
 W1_LOADS = (1, 1, 2, 1, 1, 2)
 W1_PLANES = (4, 4)
 W2_LOADS = (2, 6)
 GATE_LOADS = (2, 2, 4)
 BYTE_GATHERS = (4, 2, 2)
 WORD_GATHERS = (1, 1, 2, 2, 2)
-PART_COLS = (512, 512)
+LAST_ON_VECTOR = 192
 OUT_COLS = (128, 256, 256, 256, 128)
 
 
@@ -45,7 +48,8 @@ def tile_moe_ogt_silu_sigmoid_kernel(
     tc, x_words, x_scales, wg_words, wg_scales, w1_words, w1_scales, w2_words, w2_scales, gate, offs, out
 ):
     nc = tc.nc
-    w1_cuts, plane_cuts, w2_cuts, gate_cuts = ranges(W1_LOADS), ranges(W1_PLANES), ranges(W2_LOADS), ranges(GATE_LOADS)
+    w1_cuts, plane_cuts = ranges(W1_LOADS), ranges(W1_PLANES)
+    w2_cuts, gate_cuts = ranges(W2_LOADS), ranges(GATE_LOADS)
     byte_cuts, word_cuts = ranges(BYTE_GATHERS), ranges(WORD_GATHERS)
 
     with ExitStack() as ctx:
@@ -81,45 +85,51 @@ def tile_moe_ogt_silu_sigmoid_kernel(
         def load_token_plane(q, queue):
             rows = x_scales[0].bitcast(I32)
             queue.dma_start(
-                x_plane[32 * q : 32 * (q + 1), :].bitcast(I32), rows[4 * q : 4 * (q + 1), :].partition_broadcast(8)
+                x_plane[32 * q : 32 * (q + 1), :].bitcast(I32),
+                rows[ROWS * q : ROWS * (q + 1), :].partition_broadcast(32 // ROWS),
             )
 
-        def load_rows(plane, scales, r):
-            rows = scales.rearrange("e (q r) w -> r q e w", r=4)
-            nc.sync.dma_start(plane[r:P:32, :, :].bitcast(I32), rows[r].bitcast(I32))
+        def load_plane(plane, scales):
+            rows = scales.rearrange("e (q r) w -> r q e w", r=ROWS)
+            for r in range(ROWS):
+                nc.sync.dma_start(plane[r:P:32, :, :].bitcast(I32), rows[r].bitcast(I32))
 
-        def load_w1_rows(piece, r):
+        def load_w1_plane(piece):
             first, end = plane_cuts[piece]
-            load_rows(w1_planes[piece], w1_scales[first:end, 0], r)
+            load_plane(w1_planes[piece], w1_scales[first:end, 0])
 
-        def load_w2_rows(r):
-            load_rows(w2_plane, w2_scales[:, 0], r)
-
-        def load_wg_rows(r):
-            load_rows(wg_plane, wg_scales, r)
-
-        def load_words(tile, words):
-            nc.sync.dma_start(tile[:].bitcast(I32), words.bitcast(I32).rearrange("e p w -> p e w"))
-
-        def load_w1(piece):
-            first, end = w1_cuts[piece]
-            load_words(w1_w[piece], w1_words[first:end, 0])
-
-        def load_w2(piece):
-            first, end = w2_cuts[piece]
-            load_words(w2_w[piece], w2_words[first:end, 0])
-
-        def load_wg():
-            nc.sync.dma_start(wg_w[:].bitcast(I32), wg_words[0].bitcast(I32))
-
-        def load_x():
-            nc.sync.dma_start(x_w[:].bitcast(I32), x_words.rearrange("s p t d -> p (s t d)").bitcast(I32))
+        def load_words(tiles, cuts, words, piece):
+            first, end = cuts[piece]
+            nc.sync.dma_start(
+                tiles[piece][:].bitcast(I32), words[first:end, 0].bitcast(I32).rearrange("e p w -> p e w")
+            )
 
         def load_gate(piece):
             first, end = gate_cuts[piece]
             nc.sync.dma_start(gate_sb[piece][:], gate[:, first * C : end * C])
 
-        slot_planes, slot_words, h_couples, turned, h_turned, h_codes, h_planes, y = [{} for i in range(8)]
+        nc.sync.dma_start(offsets[:], offs)
+        for q, queue in enumerate((nc.sync, nc.sync, nc.scalar, nc.scalar)):
+            load_token_plane(q, queue)
+        nc.scalar.activation(zero_bias[:], zero_src[:], ACT.Silu)
+        nc.sync.dma_start(x_w[:].bitcast(I32), x_words.rearrange("s p t d -> p (s t d)").bitcast(I32))
+        load_words(w1_w, w1_cuts, w1_words, 0)
+        load_w1_plane(0)
+        for piece in (1, 2):
+            load_words(w1_w, w1_cuts, w1_words, piece)
+        load_w1_plane(1)
+        for piece in range(3, len(W1_LOADS)):
+            load_words(w1_w, w1_cuts, w1_words, piece)
+        load_plane(w2_plane, w2_scales[:, 0])
+        load_gate(0)
+        load_words(w2_w, w2_cuts, w2_words, 0)
+        load_plane(wg_plane, wg_scales)
+        nc.sync.dma_start(wg_w[:].bitcast(I32), wg_words[0].bitcast(I32))
+        load_words(w2_w, w2_cuts, w2_words, 1)
+        load_gate(1)
+        load_gate(2)
+
+        slot_planes, slot_words, h_couples, h_laid, h_codes, h_planes, y = [{} for i in range(7)]
 
         def slots(first, end):
             return offsets[:, first // 16 : end // 16]
@@ -134,92 +144,59 @@ def tile_moe_ogt_silu_sigmoid_kernel(
             slot_words[piece] = sbuf([P, (end - first) * C], U32, f"slot_words{piece}", tag)
             nc.vector.tensor_copy(slot_words[piece][:], x_w[:].indirect(slots(first * C, end * C)))
 
-        def first_layer(e, bank, tag=None):
+        def first_product(e, pre, first, end):
             w1_piece, w1_place = locate(w1_cuts, e)
             word_piece, word_place = locate(word_cuts, e)
             byte_piece, byte_place = locate(byte_cuts, e)
             plane_piece, plane_place = locate(plane_cuts, e)
-            pre = psum.tile([P, H], F32, name="pre", tag=bank)
             nc.tensor.matmul_mx(
-                out=pre[:],
+                out=pre,
                 lhsT=slot_words[word_piece][:, word_place * C : (word_place + 1) * C].bitcast(FP8X4),
                 lhsT_scale=slot_planes[byte_piece][:, byte_place * C : (byte_place + 1) * C],
-                rhs=w1_w[w1_piece][:, w1_place, :].bitcast(FP4X4),
-                rhs_scale=w1_planes[plane_piece][:, plane_place, :],
+                rhs=w1_w[w1_piece][:, w1_place, 2 * first : 2 * end].bitcast(FP4X4),
+                rhs_scale=w1_planes[plane_piece][:, plane_place, first:end],
                 start=True,
                 stop=True,
             )
-            h_couples[e] = sbuf([P, 2, P, 2], BF16, f"h_couples{e}", tag)
-            nc.scalar.activation(
-                h_couples[e][:], pre[:].rearrange("s (p u d) -> s u p d", u=2, d=2), ACT.Silu, bias=zero_bias[:]
-            )
 
-        def turn(g, bank):
-            turned[g] = psum.tile([P, 2, 2, C], F32, name="turned", tag=bank)
-            for place in range(2):
-                words = h_couples[2 * g + place][:].rearrange("s u p d -> s (u p d)").bitcast(F32)
-                for u in range(2):
-                    nc.tensor.transpose(turned[g][:, place, u, :], words[:, u * P : (u + 1) * P], ident[:])
-
-        def turn_beside_gate(g, banks):
-            quarter = BANK // 2
-            both = [psum.tile([P, 2, quarter], F32, name="both", tag=bank) for bank in banks]
-            cols = [slice(BANK + place * quarter, BANK + (place + 1) * quarter) for place in range(2)]
-            for place in range(2):
-                gate_product(cols[place], both[place][:, 0, :])
-            for place in range(2):
-                words = h_couples[2 * g + place][:].rearrange("s u p d -> s (u p d)").bitcast(F32)
-                for u in range(2):
-                    nc.tensor.transpose(both[place][:, 1, u * C : (u + 1) * C], words[:, u * P : (u + 1) * P], ident[:])
-            h_turned[g] = sbuf([P, 2 * H], BF16, f"h_turned{g}")
-            for place in range(2):
-                nc.vector.tensor_copy(
-                    h_turned[g][:, place * H : (place + 1) * H].bitcast(F32).rearrange("p (s u) -> p s u", u=2),
-                    both[place][:, 1, :].rearrange("p (u s) -> p s u", u=2),
-                )
-                gate_function(cols[place], both[place][:, 0, :])
-
-        def first_layer_beside_turn(e, g, banks):
-            w1_piece, w1_place = locate(w1_cuts, e)
-            word_piece, word_place = locate(word_cuts, e)
-            byte_piece, byte_place = locate(byte_cuts, e)
-            plane_piece, plane_place = locate(plane_cuts, e)
-            half = H // 2
-            both = [psum.tile([P, 2, half], F32, name="both", tag=bank) for bank in banks]
-            for place in range(2):
-                nc.tensor.matmul_mx(
-                    out=both[place][:, 0, :],
-                    lhsT=slot_words[word_piece][:, word_place * C : (word_place + 1) * C].bitcast(FP8X4),
-                    lhsT_scale=slot_planes[byte_piece][:, byte_place * C : (byte_place + 1) * C],
-                    rhs=w1_w[w1_piece][:, w1_place, place * H : (place + 1) * H].bitcast(FP4X4),
-                    rhs_scale=w1_planes[plane_piece][:, plane_place, place * half : (place + 1) * half],
-                    start=True,
-                    stop=True,
-                )
-            for place in range(2):
-                words = h_couples[2 * g + place][:].rearrange("s u p d -> s (u p d)").bitcast(F32)
-                for u in range(2):
-                    nc.tensor.transpose(both[place][:, 1, u * C : (u + 1) * C], words[:, u * P : (u + 1) * P], ident[:])
+        def new_couples(e):
             h_couples[e] = sbuf([P, 2, P, 2], BF16, f"h_couples{e}")
-            h_turned[g] = sbuf([P, 2 * H], BF16, f"h_turned{g}")
-            for place in range(2):
-                nc.scalar.activation(
-                    h_couples[e][:, :, place * P // 2 : (place + 1) * P // 2, :],
-                    both[place][:, 0, :].rearrange("s (p u d) -> s u p d", u=2, d=2),
-                    ACT.Silu,
-                    bias=zero_bias[:],
-                )
-                nc.vector.tensor_copy(
-                    h_turned[g][:, place * H : (place + 1) * H].bitcast(F32).rearrange("p (s u) -> p s u", u=2),
-                    both[place][:, 1, :].rearrange("p (u s) -> p s u", u=2),
-                )
 
-        def lay_out(g, tag=None, move=nc.vector.tensor_copy):
-            h_turned[g] = sbuf([P, 2 * H], BF16, f"h_turned{g}", tag)
-            move(
-                h_turned[g][:].bitcast(F32).rearrange("p (e s u) -> p e s u", s=C, u=2),
-                turned[g][:].rearrange("p e u s -> p e s u"),
+        def silu(into, pre):
+            nc.scalar.activation(into, pre.rearrange("s (p u d) -> s u p d", u=2, d=2), ACT.Silu, bias=zero_bias[:])
+
+        def first_layer(e, bank):
+            pre = psum.tile([P, H], F32, name="pre", tag=bank)
+            first_product(e, pre[:], 0, H)
+            new_couples(e)
+            silu(h_couples[e][:], pre[:])
+
+        def turn(e, into):
+            words = h_couples[e][:].rearrange("s u p d -> s (u p d)").bitcast(F32)
+            for u in range(2):
+                nc.tensor.transpose(into[:, u * C : (u + 1) * C], words[:, u * P : (u + 1) * P], ident[:])
+
+        def new_laid(g):
+            h_laid[g] = sbuf([P, 2 * H], BF16, f"h_laid{g}")
+
+        def lay_out(e, turned):
+            laid = h_laid[e // 2][:, (e % 2) * H : (e % 2 + 1) * H]
+            nc.vector.tensor_copy(
+                laid.bitcast(F32).rearrange("p (s u) -> p s u", u=2), turned.rearrange("p (u s) -> p s u", u=2)
             )
+
+        def turn_pair(g, bank, move):
+            turned = psum.tile([P, 2, HALF_BANK], F32, name="turned", tag=bank)
+            for place in range(2):
+                turn(2 * g + place, turned[:, place, :])
+            new_laid(g)
+            move(
+                h_laid[g][:].bitcast(F32).rearrange("p (e s u) -> p e s u", s=C, u=2),
+                turned[:].rearrange("p e (u s) -> p e s u", u=2),
+            )
+
+        def shared_banks(banks):
+            return [psum.tile([P, 2, HALF_BANK], F32, name="shared", tag=bank) for bank in banks]
 
         def quantise(g, tag=None, plane_tag=None, pieces=1):
             h_codes[g] = sbuf([P, PAIR], U32, f"h_codes{g}", tag)
@@ -228,11 +205,11 @@ def tile_moe_ogt_silu_sigmoid_kernel(
                 nc.vector.quantize_mx(
                     out=h_codes[g][:, first:end].bitcast(FP8X4),
                     scales=h_planes[g][:, first:end],
-                    in_=h_turned[g][:, 4 * first : 4 * end],
+                    in_=h_laid[g][:, 4 * first : 4 * end],
                 )
 
-        def second_layer(g, bank=None, into=None):
-            y[g] = into if bank is None else psum.tile([P, PAIR], F32, name="y", tag=bank)[:]
+        def second_layer(g, bank):
+            y[g] = psum.tile([P, BANK], F32, name="y", tag=bank)
             for place in range(2):
                 e = 2 * g + place
                 cols = slice(place * C, (place + 1) * C)
@@ -251,22 +228,23 @@ def tile_moe_ogt_silu_sigmoid_kernel(
             piece, place = locate(gate_cuts, 2 * g)
             nc.vector.scalar_tensor_tensor(
                 weighed[:, g * PAIR : (g + 1) * PAIR],
-                y[g],
+                y[g][:, :PAIR],
                 0.5,
                 gate_sb[piece][:, place * C : place * C + PAIR],
                 ALU.mult,
                 ALU.mult,
             )
 
-        def scatter_vector(first, end):
+        def scatter_on_vector(first, end):
             nc.vector.tensor_copy(by_vector[:].indirect(slots(first, end)), weighed[:, first:end])
 
-        def scatter_scalar(first, end):
+        def scatter_on_scalar(first, end):
             nc.scalar.activation(by_scalar[:].indirect(slots(first, end)), weighed[:, first:end], ACT.Copy)
 
-        def gate_product(cols, gate_pre):
+        def gate_product(v, quarter):
+            cols = slice(quarter * HALF_BANK, (quarter + 1) * HALF_BANK)
             nc.tensor.matmul_mx(
-                out=gate_pre,
+                out=v,
                 lhsT=wg_w[:].bitcast(FP4X4),
                 lhsT_scale=wg_plane[:, 0, :],
                 rhs=x_w[:, cols].bitcast(FP8X4),
@@ -275,87 +253,77 @@ def tile_moe_ogt_silu_sigmoid_kernel(
                 stop=True,
             )
 
-        def gate_function(cols, gate_pre):
-            nc.scalar.activation(gate_tanh[:, cols], gate_pre, ACT.Tanh, bias=zero_bias[:], scale=0.5)
-
-        def output_gate(first, end, bank):
-            gate_pre = psum.tile([P, end - first], F32, name="gate_pre", tag=bank)
-            gate_product(slice(first, end), gate_pre[:])
-            gate_function(slice(first, end), gate_pre[:])
-
-        def finish():
-            part = sbuf([P, T], F32, "part")
-            for first, end in ranges(PART_COLS):
-                cols = slice(first, end)
-                nc.vector.scalar_tensor_tensor(part[:, cols], gate_tanh[:, cols], 1.0, by_vector[:, cols], ALU.add, ALU.mult)
-            for first, end in ranges(OUT_COLS):
-                result = sbuf([P, end - first], F32, f"result{first}")
-                nc.vector.tensor_tensor(result[:], part[:, first:end], by_scalar[:, first:end], ALU.mult)
-                nc.sync.dma_start(out[:, first:end], result[:])
-
-        nc.sync.dma_start(offsets[:], offs)
-        load_token_plane(0, nc.sync)
-        load_token_plane(1, nc.sync)
-        load_token_plane(2, nc.scalar)
-        load_token_plane(3, nc.scalar)
-        nc.scalar.activation(zero_bias[:], zero_src[:], ACT.Silu)
-        load_x()
-        load_w1(0)
-        for r in range(4):
-            load_w1_rows(0, r)
-        load_w1(1)
-        load_w1(2)
-        for r in range(4):
-            load_w1_rows(1, r)
-        load_w1(3)
-        load_w1(4)
-        load_w1(5)
-        for r in range(4):
-            load_w2_rows(r)
-        load_gate(0)
-        load_w2(0)
-        for r in range(4):
-            load_wg_rows(r)
-        load_wg()
-        load_w2(1)
-        load_gate(1)
-        load_gate(2)
+        def half_tanh(v, quarter):
+            cols = slice(quarter * HALF_BANK, (quarter + 1) * HALF_BANK)
+            nc.scalar.activation(gate_tanh[:, cols], v, ACT.Tanh, bias=zero_bias[:], scale=0.5)
 
         gather_bytes(0)
-        for piece in range(4):
+        for piece in range(len(WORD_GATHERS) - 1):
             gather_words(piece)
         first_layer(0, "a")
         first_layer(1, "b")
         gather_bytes(1, "slot_words0")
         gather_bytes(2, "slot_words1")
-        gather_words(4, "w1_w0")
+        gather_words(len(WORD_GATHERS) - 1, "w1_w0")
         first_layer(2, "c")
         first_layer(3, "d")
-        first_layer_beside_turn(4, 0, ("a", "e"))
+
+        shared = shared_banks(("a", "e"))
+        for place in range(2):
+            first_product(4, shared[place][:, 0, :], place * HALF_BANK, (place + 1) * HALF_BANK)
+        for place in range(2):
+            turn(place, shared[place][:, 1, :])
+        new_couples(4)
+        new_laid(0)
+        for place in range(2):
+            silu(h_couples[4][:, :, place * P // 2 : (place + 1) * P // 2, :], shared[place][:, 0, :])
+            lay_out(place, shared[place][:, 1, :])
         quantise(0, pieces=2)
+
         first_layer(5, "b")
         first_layer(6, "c")
         first_layer(7, "d")
-        turn(1, "a")
-        lay_out(1)
-        turn(2, "h")
-        lay_out(2, move=nc.scalar.copy)
+        turn_pair(1, "a", nc.vector.tensor_copy)
+        turn_pair(2, "h", nc.scalar.copy)
+
         second_layer(0, "g")
         weigh(0)
-        quantise(1, "h_codes0")
-        quantise(2, None, "h_plane0")
-        scatter_scalar(0, 256)
-        output_gate(0, 512, "f")
-        turn_beside_gate(3, ("b", "c"))
+        quantise(1, tag="h_codes0")
+        quantise(2, plane_tag="h_plane0")
+        scatter_on_scalar(0, PAIR)
+
+        shared = shared_banks(("b", "c"))
+        for place in range(2):
+            gate_product(shared[place][:, 0, :], place)
+        for place in range(2):
+            turn(6 + place, shared[place][:, 1, :])
+        new_laid(3)
+        for place in range(2):
+            lay_out(6 + place, shared[place][:, 1, :])
+            half_tanh(shared[place][:, 0, :], place)
+
         second_layer(1, "e")
         weigh(1)
+        gate_product(y[1][:, PAIR:], 2)
         quantise(3)
-        scatter_scalar(256, 384)
-        scatter_vector(384, 512)
+        scatter_on_scalar(PAIR, PAIR + C)
+        half_tanh(y[1][:, PAIR:], 2)
+        scatter_on_vector(PAIR + C, 2 * PAIR)
         second_layer(2, "a")
+        gate_product(y[2][:, PAIR:], 3)
         second_layer(3, "d")
         weigh(2)
+        half_tanh(y[2][:, PAIR:], 3)
         weigh(3)
-        scatter_vector(512, 704)
-        scatter_scalar(704, 1024)
-        finish()
+        cut = 2 * PAIR + LAST_ON_VECTOR
+        scatter_on_vector(2 * PAIR, cut)
+        scatter_on_scalar(cut, T)
+
+        part = sbuf([P, T], F32, "part")
+        for first, end in ranges((T // 2, T // 2)):
+            cols = slice(first, end)
+            nc.vector.scalar_tensor_tensor(part[:, cols], gate_tanh[:, cols], 1.0, by_vector[:, cols], ALU.add, ALU.mult)
+        for first, end in ranges(OUT_COLS):
+            result = sbuf([P, end - first], F32, f"result{first}")
+            nc.vector.tensor_tensor(result[:], part[:, first:end], by_scalar[:, first:end], ALU.mult)
+            nc.sync.dma_start(out[:, first:end], result[:])

@@ -20,7 +20,7 @@ ALU = mybir.AluOpType
 
 BANK = 512
 HALF_BANK = BANK // 2
-ALIGN = 64
+ALIGN = 256
 PAIR = 2 * C
 ROWS = 4
 
@@ -70,7 +70,6 @@ def tile_moe_ogt_silu_sigmoid_kernel(
         wg_plane = sbuf([P, 1, N], U8, "wg_plane")
         gate_sb = [sbuf([P, (end - first) * C], F32, f"gate{first}") for first, end in gate_cuts]
         ident = sbuf([P, P], F32, "ident")
-        by_vector = sbuf([P, T], F32, "by_vector")
         by_scalar = sbuf([P, T], F32, "by_scalar")
         gate_tanh = sbuf([P, T], F32, "gate_tanh")
         weighed = sbuf([P, T], F32, "weighed")
@@ -79,7 +78,6 @@ def tile_moe_ogt_silu_sigmoid_kernel(
 
         nc.gpsimd.memset(zero_src[:], 0.0)
         make_identity(nc, ident[:])
-        nc.vector.memset(by_vector[:], 1.0)
         nc.vector.memset(by_scalar[:], 1.0)
 
         def load_token_plane(q, queue):
@@ -265,6 +263,8 @@ def tile_moe_ogt_silu_sigmoid_kernel(
         gather_bytes(1, "slot_words0")
         gather_bytes(2, "slot_words1")
         gather_words(len(WORD_GATHERS) - 1, "w1_w0")
+        by_vector = sbuf([P, T], F32, "by_vector", "w1_w1")
+        nc.vector.memset(by_vector[:], 1.0)
         first_layer(2, "c")
         first_layer(3, "d")
 

from contextlib import ExitStack

import concourse.mybir as mybir
from concourse.masks import make_identity

K, T, E, C, H, N = 512, 1024, 8, 128, 512, 128
P = 128
FLOPS = 2 * K * N * T + 2 * K * H * E * C + 2 * H * N * E * C

F32 = mybir.dt.float32
BF16 = mybir.dt.bfloat16
I32 = mybir.dt.int32
U32 = mybir.dt.uint32
U16 = mybir.dt.uint16
U8 = mybir.dt.uint8
FP8X4 = mybir.dt.float8_e4m3fn_x4
FP4X4 = mybir.dt.float4_e2m1fn_x4
ACT = mybir.ActivationFunctionType
ALU = mybir.AluOpType

BANK = 512
HALF_BANK = BANK // 2
ALIGN = 256
PAIR = 2 * C
ROWS = 4

W1_LOADS = (1, 1, 2, 1, 1, 2)
W1_PLANES = (4, 4)
W2_LOADS = (2, 6)
GATE_LOADS = (2, 2, 4)
BYTE_GATHERS = (4, 2, 2)
WORD_GATHERS = (1, 1, 2, 2, 2)
LAST_ON_VECTOR = 192
OUT_COLS = (128, 256, 256, 256, 128)


def ranges(sizes):
    ends = [sum(sizes[: i + 1]) for i in range(len(sizes))]
    return [(end - size, end) for size, end in zip(sizes, ends)]


def locate(cuts, e):
    piece = [first <= e < end for first, end in cuts].index(True)
    return piece, e - cuts[piece][0]


def tile_moe_ogt_silu_sigmoid_kernel(
    tc, x_words, x_scales, wg_words, wg_scales, w1_words, w1_scales, w2_words, w2_scales, gate, offs, out
):
    nc = tc.nc
    w1_cuts, plane_cuts = ranges(W1_LOADS), ranges(W1_PLANES)
    w2_cuts, gate_cuts = ranges(W2_LOADS), ranges(GATE_LOADS)
    byte_cuts, word_cuts = ranges(BYTE_GATHERS), ranges(WORD_GATHERS)

    with ExitStack() as ctx:
        held = ctx.enter_context(tc.tile_pool(name="held", bufs=1))
        psum = ctx.enter_context(tc.psum_pool(name="psum", bufs=1))

        def sbuf(shape, dtype, name, tag=None):
            return held.tile(shape, dtype, name=name, tag=tag or name, align_bytes=ALIGN)

        offsets = held.tile([P, T // 16], U16, name="offsets")
        x_w = sbuf([P, T], U32, "x_w")
        x_plane = sbuf([P, T], U8, "x_plane")
        w1_w = [sbuf([P, end - first, 2 * H], U8, f"w1_w{first}") for first, end in w1_cuts]
        w1_planes = [sbuf([P, end - first, H], U8, f"w1_plane{first}") for first, end in plane_cuts]
        w2_w = [sbuf([P, end - first, 2 * N], U8, f"w2_w{first}") for first, end in w2_cuts]
        w2_plane = sbuf([P, E, N], U8, "w2_plane")
        wg_w = sbuf([P, 2 * N], U8, "wg_w")
        wg_plane = sbuf([P, 1, N], U8, "wg_plane")
        gate_sb = [sbuf([P, (end - first) * C], F32, f"gate{first}") for first, end in gate_cuts]
        ident = sbuf([P, P], F32, "ident")
        by_scalar = sbuf([P, T], F32, "by_scalar")
        gate_tanh = sbuf([P, T], F32, "gate_tanh")
        weighed = sbuf([P, T], F32, "weighed")
        zero_src = sbuf([P, 1], F32, "zero_src")
        zero_bias = sbuf([P, 1], F32, "zero_bias")

        nc.gpsimd.memset(zero_src[:], 0.0)
        make_identity(nc, ident[:])
        nc.vector.memset(by_scalar[:], 1.0)

        def load_token_plane(q, queue):
            rows = x_scales[0].bitcast(I32)
            queue.dma_start(
                x_plane[32 * q : 32 * (q + 1), :].bitcast(I32),
                rows[ROWS * q : ROWS * (q + 1), :].partition_broadcast(32 // ROWS),
            )

        def load_plane(plane, scales):
            rows = scales.rearrange("e (q r) w -> r q e w", r=ROWS)
            for r in range(ROWS):
                nc.sync.dma_start(plane[r:P:32, :, :].bitcast(I32), rows[r].bitcast(I32))

        def load_w1_plane(piece):
            first, end = plane_cuts[piece]
            load_plane(w1_planes[piece], w1_scales[first:end, 0])

        def load_words(tiles, cuts, words, piece):
            first, end = cuts[piece]
            nc.sync.dma_start(
                tiles[piece][:].bitcast(I32), words[first:end, 0].bitcast(I32).rearrange("e p w -> p e w")
            )

        def load_gate(piece):
            first, end = gate_cuts[piece]
            nc.sync.dma_start(gate_sb[piece][:], gate[:, first * C : end * C])

        nc.sync.dma_start(offsets[:], offs)
        for q, queue in enumerate((nc.sync, nc.sync, nc.scalar, nc.scalar)):
            load_token_plane(q, queue)
        nc.scalar.activation(zero_bias[:], zero_src[:], ACT.Silu)
        nc.sync.dma_start(x_w[:].bitcast(I32), x_words.rearrange("s p t d -> p (s t d)").bitcast(I32))
        load_words(w1_w, w1_cuts, w1_words, 0)
        load_w1_plane(0)
        for piece in (1, 2):
            load_words(w1_w, w1_cuts, w1_words, piece)
        load_w1_plane(1)
        for piece in range(3, len(W1_LOADS)):
            load_words(w1_w, w1_cuts, w1_words, piece)
        load_plane(w2_plane, w2_scales[:, 0])
        load_gate(0)
        load_words(w2_w, w2_cuts, w2_words, 0)
        load_plane(wg_plane, wg_scales)
        nc.sync.dma_start(wg_w[:].bitcast(I32), wg_words[0].bitcast(I32))
        load_words(w2_w, w2_cuts, w2_words, 1)
        load_gate(1)
        load_gate(2)

        slot_planes, slot_words, h_couples, h_laid, h_codes, h_planes, y = [{} for i in range(7)]

        def slots(first, end):
            return offsets[:, first // 16 : end // 16]

        def gather_bytes(piece, tag=None):
            first, end = byte_cuts[piece]
            slot_planes[piece] = sbuf([P, (end - first) * C], U8, f"slot_plane{piece}", tag)
            nc.vector.tensor_copy(slot_planes[piece][:], x_plane[:].indirect(slots(first * C, end * C)))

        def gather_words(piece, tag=None):
            first, end = word_cuts[piece]
            slot_words[piece] = sbuf([P, (end - first) * C], U32, f"slot_words{piece}", tag)
            nc.vector.tensor_copy(slot_words[piece][:], x_w[:].indirect(slots(first * C, end * C)))

        def first_product(e, pre, first, end):
            w1_piece, w1_place = locate(w1_cuts, e)
            word_piece, word_place = locate(word_cuts, e)
            byte_piece, byte_place = locate(byte_cuts, e)
            plane_piece, plane_place = locate(plane_cuts, e)
            nc.tensor.matmul_mx(
                out=pre,
                lhsT=slot_words[word_piece][:, word_place * C : (word_place + 1) * C].bitcast(FP8X4),
                lhsT_scale=slot_planes[byte_piece][:, byte_place * C : (byte_place + 1) * C],
                rhs=w1_w[w1_piece][:, w1_place, 2 * first : 2 * end].bitcast(FP4X4),
                rhs_scale=w1_planes[plane_piece][:, plane_place, first:end],
                start=True,
                stop=True,
            )

        def new_couples(e):
            h_couples[e] = sbuf([P, 2, P, 2], BF16, f"h_couples{e}")

        def silu(into, pre):
            nc.scalar.activation(into, pre.rearrange("s (p u d) -> s u p d", u=2, d=2), ACT.Silu, bias=zero_bias[:])

        def first_layer(e, bank):
            pre = psum.tile([P, H], F32, name="pre", tag=bank)
            first_product(e, pre[:], 0, H)
            new_couples(e)
            silu(h_couples[e][:], pre[:])

        def turn(e, into):
            words = h_couples[e][:].rearrange("s u p d -> s (u p d)").bitcast(F32)
            for u in range(2):
                nc.tensor.transpose(into[:, u * C : (u + 1) * C], words[:, u * P : (u + 1) * P], ident[:])

        def new_laid(g):
            h_laid[g] = sbuf([P, 2 * H], BF16, f"h_laid{g}")

        def lay_out(e, turned):
            laid = h_laid[e // 2][:, (e % 2) * H : (e % 2 + 1) * H]
            nc.vector.tensor_copy(
                laid.bitcast(F32).rearrange("p (s u) -> p s u", u=2), turned.rearrange("p (u s) -> p s u", u=2)
            )

        def turn_pair(g, bank, move):
            turned = psum.tile([P, 2, HALF_BANK], F32, name="turned", tag=bank)
            for place in range(2):
                turn(2 * g + place, turned[:, place, :])
            new_laid(g)
            move(
                h_laid[g][:].bitcast(F32).rearrange("p (e s u) -> p e s u", s=C, u=2),
                turned[:].rearrange("p e (u s) -> p e s u", u=2),
            )

        def shared_banks(banks):
            return [psum.tile([P, 2, HALF_BANK], F32, name="shared", tag=bank) for bank in banks]

        def quantise(g, tag=None, plane_tag=None, pieces=1):
            h_codes[g] = sbuf([P, PAIR], U32, f"h_codes{g}", tag)
            h_planes[g] = sbuf([P, PAIR], U8, f"h_plane{g}", plane_tag)
            for first, end in ranges([PAIR // pieces] * pieces):
                nc.vector.quantize_mx(
                    out=h_codes[g][:, first:end].bitcast(FP8X4),
                    scales=h_planes[g][:, first:end],
                    in_=h_laid[g][:, 4 * first : 4 * end],
                )

        def second_layer(g, bank):
            y[g] = psum.tile([P, BANK], F32, name="y", tag=bank)
            for place in range(2):
                e = 2 * g + place
                cols = slice(place * C, (place + 1) * C)
                w2_piece, w2_place = locate(w2_cuts, e)
                nc.tensor.matmul_mx(
                    out=y[g][:, cols],
                    lhsT=w2_w[w2_piece][:, w2_place, :].bitcast(FP4X4),
                    lhsT_scale=w2_plane[:, e, :],
                    rhs=h_codes[g][:, cols].bitcast(FP8X4),
                    rhs_scale=h_planes[g][:, cols],
                    start=True,
                    stop=True,
                )

        def weigh(g):
            piece, place = locate(gate_cuts, 2 * g)
            nc.vector.scalar_tensor_tensor(
                weighed[:, g * PAIR : (g + 1) * PAIR],
                y[g][:, :PAIR],
                0.5,
                gate_sb[piece][:, place * C : place * C + PAIR],
                ALU.mult,
                ALU.mult,
            )

        def scatter_on_vector(first, end):
            nc.vector.tensor_copy(by_vector[:].indirect(slots(first, end)), weighed[:, first:end])

        def scatter_on_scalar(first, end):
            nc.scalar.activation(by_scalar[:].indirect(slots(first, end)), weighed[:, first:end], ACT.Copy)

        def gate_product(v, quarter):
            cols = slice(quarter * HALF_BANK, (quarter + 1) * HALF_BANK)
            nc.tensor.matmul_mx(
                out=v,
                lhsT=wg_w[:].bitcast(FP4X4),
                lhsT_scale=wg_plane[:, 0, :],
                rhs=x_w[:, cols].bitcast(FP8X4),
                rhs_scale=x_plane[:, cols],
                start=True,
                stop=True,
            )

        def half_tanh(v, quarter):
            cols = slice(quarter * HALF_BANK, (quarter + 1) * HALF_BANK)
            nc.scalar.activation(gate_tanh[:, cols], v, ACT.Tanh, bias=zero_bias[:], scale=0.5)

        gather_bytes(0)
        for piece in range(len(WORD_GATHERS) - 1):
            gather_words(piece)
        first_layer(0, "a")
        first_layer(1, "b")
        gather_bytes(1, "slot_words0")
        gather_bytes(2, "slot_words1")
        gather_words(len(WORD_GATHERS) - 1, "w1_w0")
        by_vector = sbuf([P, T], F32, "by_vector", "w1_w1")
        nc.vector.memset(by_vector[:], 1.0)
        first_layer(2, "c")
        first_layer(3, "d")

        shared = shared_banks(("a", "e"))
        for place in range(2):
            first_product(4, shared[place][:, 0, :], place * HALF_BANK, (place + 1) * HALF_BANK)
        for place in range(2):
            turn(place, shared[place][:, 1, :])
        new_couples(4)
        new_laid(0)
        for place in range(2):
            silu(h_couples[4][:, :, place * P // 2 : (place + 1) * P // 2, :], shared[place][:, 0, :])
            lay_out(place, shared[place][:, 1, :])
        quantise(0, pieces=2)

        first_layer(5, "b")
        first_layer(6, "c")
        first_layer(7, "d")
        turn_pair(1, "a", nc.vector.tensor_copy)
        turn_pair(2, "h", nc.scalar.copy)

        second_layer(0, "g")
        weigh(0)
        quantise(1, tag="h_codes0")
        quantise(2, plane_tag="h_plane0")
        scatter_on_scalar(0, PAIR)

        shared = shared_banks(("b", "c"))
        for place in range(2):
            gate_product(shared[place][:, 0, :], place)
        for place in range(2):
            turn(6 + place, shared[place][:, 1, :])
        new_laid(3)
        for place in range(2):
            lay_out(6 + place, shared[place][:, 1, :])
            half_tanh(shared[place][:, 0, :], place)

        second_layer(1, "e")
        weigh(1)
        gate_product(y[1][:, PAIR:], 2)
        quantise(3)
        scatter_on_scalar(PAIR, PAIR + C)
        half_tanh(y[1][:, PAIR:], 2)
        scatter_on_vector(PAIR + C, 2 * PAIR)
        second_layer(2, "a")
        gate_product(y[2][:, PAIR:], 3)
        second_layer(3, "d")
        weigh(2)
        half_tanh(y[2][:, PAIR:], 3)
        weigh(3)
        cut = 2 * PAIR + LAST_ON_VECTOR
        scatter_on_vector(2 * PAIR, cut)
        scatter_on_scalar(cut, T)

        part = sbuf([P, T], F32, "part")
        for first, end in ranges((T // 2, T // 2)):
            cols = slice(first, end)
            nc.vector.scalar_tensor_tensor(part[:, cols], gate_tanh[:, cols], 1.0, by_vector[:, cols], ALU.add, ALU.mult)
        for first, end in ranges(OUT_COLS):
            result = sbuf([P, end - first], F32, f"result{first}")
            nc.vector.tensor_tensor(result[:], part[:, first:end], by_scalar[:, first:end], ALU.mult)
            nc.sync.dma_start(out[:, first:end], result[:])
